import numpy as np, ml_dtypes
CORES = [48,51,52,55]
N = 4
BF = ml_dtypes.bfloat16
def gentries(a):
    return np.ascontiguousarray(a.reshape(8, 16, -1).transpose(0, 2, 1)).reshape(8, -1)
def gtable(e):
    e = np.asarray(e); return np.ascontiguousarray(e.reshape(8, -1, 16).transpose(0, 2, 1)).reshape(128, -1).astype(np.int32)
W, P, R, S, E, LM = 3072, 256, 4, 1, 1, 14
def pack(nb, x, v, z, th):
    return {"nb": np.ascontiguousarray(nb.reshape(N, 128, W)).astype(np.int32), "xd": np.ascontiguousarray(x.reshape(N, 128, W)).astype(np.float32).astype(BF),
            "pv": np.stack([gtable(a) for a in v]), "pz": np.ascontiguousarray(z.reshape(N, 128, P)).astype(np.float32).astype(BF), "th": np.repeat(th, 16, axis=1).astype(np.int32)}
def blur(rng, pat, sel, m):
    b = np.stack([pat[g][sel[:, g]] for g in range(8)], axis=1).transpose(0, 1, 3, 2)
    b = np.clip(b + rng.integers(-1, 2, b.shape) * (rng.random(b.shape) < 0.25), 0, 15)
    return np.where(np.arange(16)[:, None] < m[:, :, None, :], b, rng.integers(0, 16, b.shape))
def alike(rng, s, want):
    o = np.argsort(s, kind="stable"); n = np.bincount(s, minlength=8); b = np.add.accumulate(n) - n
    return o[np.minimum(b[want] + (rng.random(want.shape) * n[want]).astype(np.int64), len(s) - 1)]
def parts(rng):
    pat = rng.integers(0, 16, (8, 8, 16))
    s = np.where(rng.random((N, 8, W)) < 0.7, rng.integers(0, 8, (1, 8, W)), rng.integers(0, 8, (N, 8, W)))
    x = blur(rng, pat, s, rng.integers(0, 17, (N, 8, W)))
    sp = rng.integers(0, 8, (N, 8, P)); z = blur(rng, pat, sp, rng.integers(0, 17, (N, 8, P)))
    nb = rng.integers(0, W, (N, 8, 16, W)); v = rng.integers(0, W, (N, 8, P))
    for q in range(N):
        for g in range(8):
            w = alike(rng, s[q, g], np.broadcast_to(s[q, g], (16, W)))
            nb[q, g] = np.where(rng.random((16, W)) < 0.5, w, nb[q, g])
            v[q, g] = np.where(rng.random(P) < 0.6, alike(rng, s[q, g], sp[q, g]), v[q, g])
    th = np.stack([rng.integers(40, 91, (N, 8)), rng.integers(25, 76, (N, 8))], axis=-1)
    return nb, x, v, z, th
def setup_inputs(rng):
    return pack(*parts(rng))
def uneven(rng, shape, n):
    a = np.minimum((n * rng.random(shape) ** 3).astype(np.int64), n - 1)
    return np.where(rng.random(shape[:-1] + (1,)) < 0.5, a, n - 1 - a)
def setup_inputs_spread(rng):
    def digits(n):
        top = 1 << rng.integers(0, 5, (N, 8, 1, n)); a = np.minimum((rng.random((N, 8, 16, n)) * top).astype(np.int64), 15)
        return np.where(rng.random((N, 8, 1, n)) < 0.5, a, 15 - a)
    return pack(uneven(rng, (N, 8, 16, W), W), digits(W), uneven(rng, (N, 8, P), W), digits(P), rng.integers(0, 242, (N, 8, 2)))
def setup_inputs_ends(rng):
    def digits(n):
        return np.where(rng.random((N, 8, 1, n)) < 0.5, 15 * rng.integers(0, 2, (N, 8, 1, n)), 15 * rng.integers(0, 2, (N, 8, 16, n)))
    x = digits(W); x[..., 0] = 0; x[..., W - 1] = 15; x[:, 1:6:2, :, 0] = 15; x[:, 1:6:2, :, W - 1] = 0
    z = digits(P); z[..., 0] = 0; z[..., 1] = 15; z[..., P - 2] = 15; z[..., P - 1] = 0
    nb = np.where(rng.random((N, 8, 16, W)) < 0.25, rng.integers(0, W, (N, 8, 16, W)), (W - 1) * rng.integers(0, 2, (N, 8, 16, W)))
    nb[:, 7, :, W - 1] = W - 1
    v = np.where(rng.random((N, 8, P)) < 0.25, rng.integers(0, W, (N, 8, P)), (W - 1) * rng.integers(0, 2, (N, 8, P)))
    v[..., 0] = 0; v[..., 1] = W - 1; v[..., P - 2] = W - 1; v[..., P - 1] = W - 1
    pairs = np.array([[0, 0], [0, 241], [241, 0], [241, 241]])
    th = pairs[np.argsort(rng.random((N, 8)), axis=1) & 3]; th[N - 1] = pairs[np.array([0, 3, 2, 1, 0, 2, 3, 1])]; th[:, 2] = np.array([120, 121])
    return pack(nb, x, v, z, th)
def setup_inputs_corners(rng):
    M = P // 4; nb = np.zeros((N, 8, 16, W), np.int64); x = np.zeros((N, 8, 16, W), np.int64); v = np.zeros((N, 8, P), np.int64); z = np.zeros((N, 8, 16, P), np.int64)
    th = np.zeros((N, 8, 2), np.int64); th[..., 0] = 40; th[..., 1] = 24
    rows = np.arange(16)[:, None]
    for q in range(N):
        for g in range(8):
            zz = rng.integers(4, 12, 16)[:, None]; o = rng.permutation(W); place = o[:P]; cont = o[P:P + 16 * M].reshape(M, 16); good = o[P + 16 * M::2]; miss = o[P + 16 * M + 1::2]
            lw = rng.choice(np.array([0, 1, 2, 7, LM - 1, LM, LM + 1, 15, 16]), P); lv = np.minimum(lw, LM)[:M]; case = rng.permutation(np.arange(M) & 7)
            d = np.zeros(W, np.int64); d[good] = rng.choice(np.array([0, 1, 23]), len(good)); d[miss] = rng.choice(np.array([24, 24, 25, 39, 40]), len(miss))
            d[cont] = rng.choice(np.array([40, 40, 41, 54, 55, 56]), (M, 16)); j = np.flatnonzero(case == 0); d[cont[j, lv[j]]] = 39
            sign = 1 - 2 * rng.integers(0, 2, (16, W)); diff = (d >> 4) + (np.argsort(rng.random((16, W)), axis=0) < (d & 15))
            diff[:, place] = np.where(rows < lw, rng.integers(0, 2, (16, P)), np.where(rows == lw, 2, rng.integers(0, 5, (16, P))))
            x[q, g] = zz + sign * diff
            w = rng.random((16, W)); b = np.where(w < 0.15, np.arange(W), np.where(w < 0.25, 0, np.where(w < 0.35, W - 1, rng.integers(0, W, (16, W)))))
            b[:, place[:M]] = cont.T
            for e in range(E + 1): b[(lv + e)[:, None], cont] = rng.choice(miss, (M, 16))
            last = (lv + 15) & 15
            for c, e, k in ((1, 0, last), (2, 0, lv), (3, 1, last), (4, E, lv), (6, 0, last), (7, 0, 0 * lv + 15), (7, 0, 0 * lv)):
                j = np.flatnonzero(case == c); b[lv[j] + e, cont[j, k[j]]] = rng.choice(good, len(j))
            j = np.flatnonzero(case == 6); b[(lv[j] + 1)[:, None], cont[j]] = rng.choice(good, (len(j), 16))
            nb[q, g] = b
            pl = place.copy(); n = P - M; pl[M:] = np.where(rng.random(n) < 0.25, rng.choice(place[:M], n), pl[M:]); pl[P - 1] = W - 1; pl[P - 2] = 0
            t = np.repeat(zz, P, axis=1); t[:, M:] = np.where(rng.random(n) < 0.5, np.clip(zz + rng.integers(-3, 4, (16, n)), 0, 15), rng.integers(0, 16, (16, n)))
            r = rng.permutation(P); v[q, g] = pl[r]; z[q, g] = t[:, r]
    th[1, :, 0] = 0; th[N - 1, :4] = np.array([[0, 0], [0, 241], [241, 0], [241, 241]])
    return pack(nb, x, v, z, th)
def setup_inputs_crowd(rng):
    nb, x, v, z, th = parts(rng)
    v[:, 0] = rng.integers(0, W, (N, 1)); v[:, 1] = rng.integers(0, W - 1, (N, 1))
    for q in range(N): v[q, 1, rng.integers(0, P)] = W - 1
    v[:, 2] = rng.choice(np.array([0, 3, W // 2, W - 1]), (N, P)); v[:, 3] = np.repeat(v[:, 3, :P // 2], 2, axis=1)
    nb[:, 4, :15] = rng.integers(0, W, (N, 1, 1)); nb[:, 5] = nb[:, 5, :1]
    v[:, 6] = rng.integers(0, W, (N, 1)); z[:, 6] = z[:, 6, :, :1]; v[:, 7] = W - 1
    th[0, :, 0] = 0; th[1, :, 0] = 0; th[1, 7, 0] = 1
    x[1, 7, 15] = np.minimum(x[1, 7, 15], 14); z[1, 7, 15] = 15; j = rng.integers(0, P); u = rng.integers(0, W - 1)
    nb[1, 7, :, v[1, 7, j]] = u; z[1, 7, :, j] = x[1, 7, :, u]
    th[2, :7, 0] = 241; th[2, 7, 0] = 0
    return pack(nb, x, v, z, th)
def setup_inputs_calm(rng):
    M = P - P // 8; rows = np.arange(16)[:, None]
    nb = rng.integers(0, W, (N, 8, 16, W)); x = rng.integers(0, 16, (N, 8, 16, W))
    n = np.argsort(rng.random((8, W)), axis=1)[:, :(R + 1) * M].reshape(8, R + 1, M)
    th = np.zeros((N, 8, 2), np.int64); th[..., 0] = rng.integers(16, 33, (N, 8))
    z0 = np.clip(rng.integers(0, 16, (8, 16, M)) + rng.integers(-1, 2, (N, 8, 16, M)), 0, 15); z = z0
    at = np.where(rows < rng.integers(0, 17, (N, 8, 1, M)), np.clip(z + rng.integers(-1, 2, z.shape), 0, 15), rng.integers(0, 16, z.shape))
    o = rng.permutation(N); want = np.zeros((R - 1, N), np.int64)
    for t in range(R - 1): want[t, o] = (np.arange(N) + t) & 3
    want[0, o[0]] = 8 * P; want[0, o[1]] = 8 * P - 1
    weight = 1 + (np.arange(M) < P - M).astype(np.int64); a = np.zeros(N, np.int64)
    for t in range(R):
        if t > 0: z = np.roll(z, S, axis=0)
        near = (np.abs(at - z) <= 1).astype(np.int64)
        l = np.minimum(np.add.reduce(np.multiply.accumulate(near, axis=2), axis=2), LM)
        for q in range(N):
            for g in range(8):
                x[q, g][:, n[g, t]] = at[q, g]; nb[q, g][l[q, g], n[g, t]] = n[g, t + 1]
                if t < R - 1: nb[q, g][15, n[g, t]] = n[g, t + 1]
        fail = rng.random((N, 8, M)) < 0.4; over = np.where(rng.random((N, 8, M)) < 0.5, 0, rng.integers(0, 8, (N, 8, M)))
        if t < R - 1:
            over = 0 * over
            for q in range(N):
                k = int(want[t, q]); j = rng.permutation(8 * (2 * M - P))[:min(k, 8 * P - k)]
                fail[q] = k > 3; fail[q, j & 7, P - M + (j >> 3)] = k < 4
        h = th[..., 0][:, :, None] + (a & 15)[:, None, None]
        under = np.where(rng.random((N, 8, M)) < 0.5, 0, rng.integers(0, 16, (N, 8, M)))
        need = np.where(fail, h + over, h - 1 - under)[:, :, None, :]
        m = rng.integers(0, 10, (N, 8, 1, M)); base = need // (16 - m)
        place = np.argsort(np.argsort(rng.random(z.shape) + 2 * (rows < m), axis=2), axis=2)
        diff = np.where(rows >= m, base + (place < need - base * (16 - m)), 0)
        come = z + np.where(z < 8, diff, -diff)
        a = np.add.reduce((fail * weight).reshape(N, -1), axis=1)
        z = np.where(fail[:, :, None, :], np.abs(z - at), z); at = come
    v = np.zeros((N, 8, P), np.int64); zp = np.zeros((N, 8, 16, P), np.int64); who = np.concatenate([np.arange(M), np.arange(P - M)])
    for q in range(N):
        for g in range(8):
            x[q, g][:, n[g, R]] = at[q, g]
            r = who[rng.permutation(P)]; v[q, g] = n[g, 0][r]; zp[q, g] = z0[q, g][:, r]
    return pack(nb, x, v, zp, th)
def check_inputs(d):
    bad = []
    for k, hi in (("nb", W - 1), ("xd", 15), ("pv", W - 1), ("pz", 15), ("th", 241)):
        a = np.asarray(d[k]).astype(np.float64)
        if not (np.min(a) >= 0 and np.max(a) <= hi): bad.append("range of " + k)
        if np.any(a != np.floor(a)): bad.append("whole numbers of " + k)
    t = np.asarray(d["th"]).reshape(N, 8, 16, 2)
    if np.any(t != t[:, :, :1]): bad.append("rows of a group alike in th")
    return bad
def dist(x, z, u):
    s = np.zeros(u.shape, np.int64)
    for p in range(16):
        s = s + np.abs(np.take_along_axis(x[:, :, p], u.reshape(N, 8, -1), 2).reshape(u.shape) - z[:, :, p][:, :, None, :])
    return s
def reference(nb, xd, pv, pz, th):
    c = nb.astype(np.int64).reshape(N, 8, 16, W); x = xd.astype(np.float32).astype(np.int64).reshape(N, 8, 16, W)
    v = np.stack([gentries(a) for a in pv]).astype(np.int64); z = pz.astype(np.float32).astype(np.int64).reshape(N, 8, 16, P)
    h = th.astype(np.int64).reshape(N, 8, 16, 2)[:, :, 0]; a = np.zeros(N, np.int64)
    for t in range(R):
        if t > 0: v = np.roll(v, S, axis=0); z = np.roll(z, S, axis=0)
        xv = np.take_along_axis(x, v[:, :, None, :], 3); con = np.take_along_axis(c, v[:, :, None, :], 3)
        near = (np.abs(xv - z) <= 1).astype(np.int64)
        l = np.minimum(np.add.reduce(np.multiply.accumulate(near, axis=2), axis=2), LM)
        tl = np.take_along_axis(con, l[:, :, None, :], 2)
        ok = dist(x, z, tl)[:, :, 0] < h[:, :, 0, None] + (a & 15)[:, None, None]
        new = np.where(ok, tl[:, :, 0], con[:, :, 15]); todo = ~ok; fixed = np.zeros(ok.shape, bool)
        order = (l[:, :, None, :] + np.arange(16)[:, None]) & 15
        for e in range(E + 1):
            cand = np.take_along_axis(c.reshape(N, 8, 16 * W), ((l + e)[:, :, None, :] * W + con).reshape(N, 8, -1), 2).reshape(N, 8, 16, P)
            hit = np.take_along_axis(dist(x, z, cand) < h[:, :, 1, None, None], order, 2); cand = np.take_along_axis(cand, order, 2)
            got = todo & np.any(hit, axis=2)
            new = np.where(got, np.take_along_axis(cand, np.argmax(hit, axis=2)[:, :, None, :], 2)[:, :, 0], new)
            fixed = fixed | got; todo = todo & ~got
        a = np.add.reduce((~ok).astype(np.int64).reshape(N, -1), axis=1)
        for q in range(N):
            for g in range(8):
                i = np.flatnonzero(fixed[q, g]); u, k = np.unique(v[q, g, i], return_index=True); i = i[k]
                c[q, g][l[q, g][i], u] = new[q, g][i]
                if t < R - 1:
                    u, i = np.unique(v[q, g], return_index=True)
                    x[q, g][:, u] = (xv[q, g][:, i] + z[q, g][:, i]) >> 1
        z = np.where(todo[:, :, None, :], np.abs(z - xv), z); v = new
    return {"ynb": c.reshape(N, 128, W).astype(np.float32), "yv": np.stack([gtable(b) for b in v]).astype(np.float32), "yz": z.reshape(N, 128, P).astype(np.float32).astype(BF)}

@@ -1,0 +1,521 @@
+import numpy as np
+from concourse.mybir import dt, AluOpType, AxisListType, ActivationFunctionType
+
+W = 3072
+WT = W + 256
+
+SCRATCH = {
+    "nbI": ("sbuf", [128, W], "int32"), "nbS": ("sbuf", [128, WT], "float32"), "xdS": ("sbuf", [128, WT], "bfloat16"),
+    "idW": ("sbuf", [128, W], "float32"), "yn": ("sbuf", [128, W], "float32"),
+    "E30": ("sbuf", [128, 16, 256], "bfloat16"), "E31": ("sbuf", [128, 16, 256], "bfloat16"),
+    "TRI": ("sbuf", [128, 16, 16], "bfloat16"),
+}
+
+
+def _decl():
+    for names, cols, d in (("maskE zE xg", 4096, "bfloat16"), ("mk", 4096, "float16"), ("dd", 8192, "bfloat16"), ("LQ", 2048, "bfloat16"),
+                           ("dz adz nn nm Pb m2 ohb dlt d0 hb2 junk W0 cb crb xn", 256, "bfloat16"), ("Wt hw fi", 512, "bfloat16"),
+                           ("VB co hc lc", 256, "float16"), ("fc pk", 512, "float16"), ("conF wv rr", 256, "float32"),
+                           ("conU", 256, "uint16"), ("cU", 512, "uint16"), ("TLu offA offR", 16, "uint16"),
+                           ("vS rp q1 o1 o2 o3 yvS tr trS", 16, "float32"), ("pvI", 16, "int32"), ("xi", 256, "int32"),
+                           ("thI", 2, "int32"), ("thF", 2, "float32"), ("bB", 1, "float32"), ("Hc hs", 4, "float32"),
+                           ("hsb", 4, "bfloat16"), ("hi0 hi1", 4, "int32"), ("pI pB", 8, "int32"), ("pC", 32, "float32"),
+                           ("ones ZZ ta tb ZB0", 144, "bfloat16"), ("ZFe ZFo ZFa ZF0", 144, "float16"),
+                           ("BLKb D0 D1 D2 CA CB D0n mt M1 M2 M2a In Ih B7 AW VW ALT", 128, "bfloat16"),
+                           ("BF1 BFh BF15", 128, "float16"),
+                           ("VL0 VL1 VL2 VL3 VN0 VN1 VN2 VN3", 16, "uint16"), ("z0 z1 z2 z3 zn0 zn1 zn2 zn3", 256, "bfloat16")):
+        for n in names.split():
+            SCRATCH[n] = ("sbuf", [128, cols], d)
+    for b in range(8):
+        SCRATCH["ps%d" % b] = ("psum", [128, 512], "float32")
+
+
+_decl()
+DMAS = ["pv", "pz", "th", "xa", "xb", "n0", "n1", "n2", "n3", "y0", "y1", "y2", "y3", "yv", "yz0", "yz1"]
+SEMAPHORES = ["sV", "sS", "sP", "sG", "loc"] + ["d_" + d for d in DMAS] + ["a%s%d" % (n, t) for n in ("l", "y", "z") for t in range(4)]
+
+
+def rank_program(g, core, T, topo):
+    rank = T.rank_of(core)
+    if rank is None:
+        return
+    A, F = AluOpType, ActivationFunctionType
+    ENG = {"V": g.vector, "S": g.scalar, "P": g.tensor, "G": g, "Y": g.sync}
+    cnt = {"sV": 0, "sS": 0, "sP": 0, "sG": 0}
+    known = {q: {} for q in ENG}
+    snap = {}
+    rec = {}
+
+    def need(q, name, lo, hi, wr, out):
+        ps = name[:2] == "ps"
+        for (a, b, q2, s, c, w2) in rec.get(name, ()):
+            if (ps and q2 != q) or (a < hi and lo < b and (wr or w2)):
+                if out.get(s, 0) < c:
+                    out[s] = c
+
+    def note(q, name, lo, hi, s, c, wr):
+        keep = []
+        for x in rec.get(name, []):
+            inside = lo <= x[0] and x[1] <= hi
+            if inside and (wr or (x[2] == q and not x[5] and x[3] == s)):
+                continue
+            keep.append(x)
+        keep.append((lo, hi, q, s, c, wr))
+        rec[name] = keep
+
+    def waits(q, deps):
+        k = known[q]
+        for s in sorted(deps, key=lambda s: -len(snap.get((s, deps[s]), ()))):
+            c = deps[s]
+            if k.get(s, 0) >= c:
+                continue
+            ENG[q].wait_ge(T.sem[s], c)
+            for s2, c2 in snap.get((s, c), {}).items():
+                if k.get(s2, 0) < c2:
+                    k[s2] = c2
+            k[s] = max(k.get(s, 0), c)
+
+    def op(q, emit, reads, writes, sem=None, inc=1):
+        deps = {}
+        for x in reads:
+            need(q, x[1], x[2], x[3], False, deps)
+        for x in writes:
+            need(q, x[1], x[2], x[3], True, deps)
+        waits(q, deps)
+        r = emit(ENG[q])
+        if sem is None:
+            s = "s" + q
+            cnt[s] += 1
+            c = cnt[s]
+        else:
+            s, c = sem, inc
+        r.then_inc(T.sem[s], inc)
+        snap[(s, c)] = dict(known[q])
+        for x in reads:
+            note(q, x[1], x[2], x[3], s, c, False)
+        for x in writes:
+            note(q, x[1], x[2], x[3], s, c, True)
+
+    def X(n, a=0, b=None, st=1):
+        if b is None:
+            b = SCRATCH[n][1][1]
+        return (T[n][:, a:b:st] if st > 1 else T[n][:, a:b], n, a, b)
+
+    def IND(win, off):
+        return (win[0].indirect(off[0]), win, off)
+
+    def rd(x):
+        return [x[1], x[2]] if len(x) == 3 else [x]
+
+    def tt(out, a, b, o):
+        op("V", lambda e: e.tensor_tensor(out[0], a[0], b[0], o), rd(a) + rd(b), [out])
+
+    def ts(out, a, s1, o0, s2=None, o1=None):
+        reads = rd(a)
+        v1, v2 = s1, s2
+        if isinstance(s1, tuple):
+            reads = reads + [s1]; v1 = s1[0]
+        if isinstance(s2, tuple):
+            reads = reads + [s2]; v2 = s2[0]
+        if o1 is None:
+            op("V", lambda e: e.tensor_scalar(out[0], a[0], v1, None, o0), reads, [out])
+        else:
+            op("V", lambda e: e.tensor_scalar(out[0], a[0], v1, v2, o0, o1), reads, [out])
+
+    def cp(out, a):
+        if len(out) == 3:
+            op("V", lambda e: e.tensor_copy(out[0], a[0]), rd(a) + [out[2]], [out[1]])
+        else:
+            op("V", lambda e: e.tensor_copy(out[0], a[0]), rd(a), [out])
+
+    def act(out, a, f, bias=None, scale=None, acc=None):
+        kw = {}
+        reads, writes = rd(a), [out]
+        for nm, v in (("bias", bias), ("scale", scale)):
+            if v is not None:
+                if isinstance(v, tuple):
+                    reads = reads + [v]; kw[nm] = v[0]
+                else:
+                    kw[nm] = v
+        if acc is not None:
+            writes = writes + [acc]; kw["accum_out"] = acc[0]
+        op("S", lambda e: e.activation(out[0], a[0], f, **kw), reads, writes)
+
+    def scp(out, a):
+        act(out, a, F.Copy)
+
+    def mms(items):
+        deps = {}
+        for (o, l, r) in items:
+            need("P", o[1], o[2], o[3], True, deps)
+            need("P", l[1], l[2], l[3], False, deps)
+            need("P", r[1], r[2], r[3], False, deps)
+        waits("P", deps)
+        n = len(items)
+        for j, (o, l, r) in enumerate(items):
+            g.tensor.matmul(o[0], l[0], r[0], j == 0, j == n - 1).then_inc(T.sem.sP, 1)
+        cnt["sP"] += n
+        c = cnt["sP"]
+        snap[("sP", c)] = dict(known["P"])
+        for (o, l, r) in items:
+            note("P", l[1], l[2], l[3], "sP", c, False)
+            note("P", r[1], r[2], r[3], "sP", c, False)
+        for (o, l, r) in items:
+            note("P", o[1], o[2], o[3], "sP", c, True)
+
+    def dma(q, out, oacc, in_, iacc, name):
+        op(q, lambda e: e.dma_start(out, in_), iacc, oacc, sem="d_" + name, inc=16)
+
+    def iota(x, pat, base, cm):
+        kw = {} if SCRATCH[x[1]][2] == "int32" else {"allow_small_or_imprecise_dtypes": True}
+        op("G", lambda e: e.iota(x[0], pat, base, cm, **kw), [], [x])
+
+    def sel(out, a, pat, o, base, cm):
+        op("G", lambda e: e.affine_select(out[0], a[0], pat, o, 0.0, base, cm), [a], [out])
+
+    C4, H2 = W // 4, W // 2
+    dma("Y", T.pvI[:, :], [X("pvI")], T.pv[:, :], [], "pv")
+    dma("S", T.z0[:, :], [X("z0")], T.pz[:, :], [], "pz")
+    dma("Y", T.xdS[:, 0:H2], [X("xdS", 0, H2)], T.xd[:, 0:H2], [], "xa")
+    dma("S", T.xdS[:, H2:W], [X("xdS", H2, W)], T.xd[:, H2:W], [], "xb")
+    for j in range(4):
+        a, b = j * C4, (j + 1) * C4
+        dma("Y" if j % 2 == 0 else "S", T.nbI[:, a:b], [X("nbI", a, b)], T.nb[:, a:b], [], "n%d" % j)
+    dma("Y", T.thI[:, :], [X("thI")], T.th[:, :], [], "th")
+
+    pc = lambda j: X("pC", j, j + 1)
+    iota(X("pI", 0, 1), [[1, 1]], 0, 1)
+    op("V", lambda e: e.memset(T.ones[:, :], 1.0), [], [X("ones")])
+    op("V", lambda e: e.memset(T.AW[:, :], 1.0 / 32), [], [X("AW")])
+    ts(X("pI", 1, 2), X("pI", 0, 1), 15, A.bitwise_and)
+    cp(pc(0), X("pI", 1, 2))
+    for b in range(4):
+        ts(X("pB", b, b + 1), X("pI", 1, 2), b, A.arith_shift_right, 1, A.bitwise_and)
+    cp(X("pC", 1, 5), X("pB", 0, 4))
+    for b in range(4):
+        ts(pc(5 + b), pc(1 + b), 2.0 ** -(1 << b) - 1.0, A.mult, 1.0, A.add)
+    tt(pc(9), pc(5), pc(6), A.mult)
+    tt(pc(10), pc(7), pc(8), A.mult)
+    tt(pc(11), pc(9), pc(10), A.mult)
+    ts(pc(13), pc(0), 14.0, A.is_lt)
+    ts(pc(14), pc(0), 14.0, A.is_equal)
+    ts(pc(15), pc(0), 15.0, A.is_equal)
+    ts(pc(16), pc(11), 32768.0, A.mult)
+    tt(pc(17), pc(16), pc(13), A.mult)
+    tt(pc(18), pc(17), pc(14), A.subtract)
+    ts(pc(19), pc(15), 1.0e9, A.mult)
+    tt(pc(20), pc(18), pc(19), A.add)
+    ts(pc(21), pc(1), -2.0, A.mult, 1.0, A.add)
+    tt(pc(22), pc(21), pc(13), A.mult)
+    ts(pc(23), pc(15), -1.0, A.mult, 1.0, A.add)
+    tt(pc(27), pc(11), pc(23), A.mult)
+    ts(pc(12), pc(27), 2.0 ** -16 - 1.0, A.mult)
+    ts(pc(24), pc(1), -1.0, A.mult, 1.0, A.add)
+    ts(pc(25), pc(0), 0.0, A.is_equal)
+    ts(pc(26), pc(25), 4096.0, A.mult)
+    sel(X("ta", 0, 128), X("ones", 0, 128), [[-16, 8], [0, 16]], A.is_ge, 0, 1)
+    sel(X("BLKb"), X("ta", 0, 128), [[16, 8], [0, 16]], A.is_ge, 15, -1)
+    for n, j in (("VW", 17), ("ALT", 22)):
+        ts(X(n), X("BLKb"), pc(j), A.mult)
+    for n, b in (("D0", 0), ("D2", 2), ("CA", -15), ("CB", -14), ("D1", 1)):
+        sel(X(n), X("BLKb"), [[-1, 128]], A.is_equal, b, 1)
+    ts(X("D0n"), X("D0"), pc(23), A.mult)
+    tt(X("mt"), X("CA"), X("D0n"), A.subtract)
+    tt(X("M2a"), X("D2"), X("CB"), A.add)
+    tt(X("M2"), X("M2a"), X("mt"), A.add)
+    tt(X("M1"), X("D1"), X("mt"), A.add)
+    sel(X("ta"), X("ones"), [[-16, 9], [0, 16]], A.is_ge, 0, 1)
+    sel(X("tb"), X("ta"), [[16, 9], [0, 16]], A.is_ge, 15, -1)
+    sel(X("ZZ"), X("tb"), [[0, 9], [1, 16]], A.is_equal, -15, 0)
+    iota(X("idW"), [[1, W]], -1536, 0)
+    iota(X("rr"), [[0, 16], [1, 16]], 0, 0)
+    iota(X("tr"), [[16, 16]], W - 1536, 0)
+    cp(X("VL0"), X("pvI"))
+
+    def consts_b():
+        ts(X("ZFe"), X("ZZ"), pc(24), A.mult)
+        ts(X("ZFo"), X("ZZ"), pc(1), A.mult)
+        cp(X("ZFa"), X("ZZ"))
+        ts((T.TRI[:, :, :], "TRI", 0, 256), X("rr"), pc(0), A.is_gt)
+
+    def consts_c():
+        ts(X("ZF0"), X("ZZ"), pc(25), A.mult)
+        ts(X("ZB0"), X("ZZ"), pc(26), A.mult)
+        ts(X("In"), X("D0"), -1.0, A.mult)
+        ts(X("Ih"), X("D0"), 0.5, A.mult)
+        ts(X("B7"), X("BLKb"), 0.4375, A.mult)
+        cp(X("BF1"), X("BLKb"))
+        ts(X("BFh"), X("BLKb"), 0.5, A.mult)
+        ts(X("BF15"), X("BLKb"), pc(15), A.mult)
+        ts(X("trS"), X("tr"), pc(0), A.add)
+        cp(X("thF"), X("thI"))
+        cp(X("Hc", 0, 1), X("thF", 0, 1))
+        ts(X("bB"), X("thF", 1, 2), 2.0, A.mult, -1.0, A.add)
+
+    nxt = T.cores[(rank + 1) % len(T.cores)]
+    prv = T.cores[(rank - 1) % len(T.cores)]
+    adr = topo.addr(nxt)
+    eng = topo.engines(core, nxt)
+    half = len(eng) // 2
+    m_lo, m_hi = sum(1 << e for e in eng[:half]), sum(1 << e for e in eng[half:])
+    n_in = len(topo.engines(prv, core)) // 2
+    loc = [0]
+
+    def send(dst, src, sem, m):
+        deps = {}
+        need("G", src[1], src[2], src[3], False, deps)
+        waits("G", deps)
+        g.remote_dma(dst, src[0], T.sem[sem], T.sem.loc, adr[1], adr[0], m)
+        loc[0] += half
+
+    def expand(copy, dst, src, i0, i1):
+        a, b = 16 * i0, 16 * i1
+        copy(X(dst, a, b, 16), X(src, i0, i1))
+        for k in (8, 4, 2, 1):
+            copy(X(dst, a + k, b, 2 * k), X(dst, a, b, 2 * k))
+
+    def ind_x(off):
+        return IND(X("xdS", 0, W), off)
+
+    def ind_n(off):
+        return IND(X("nbS", 0, W), off)
+
+    def erow(E, q):
+        return (T[E][:, q, 0:256 - 16 * q], E, 256 * q, 240 * q + 256)
+
+    def count(ps, lhs, E):
+        mms([(X(ps, 16 * q, 256), lhs(q), erow(E, q)) for q in range(16)])
+
+    def to_list(ps, src):
+        mms([(X(ps, 480, 496), X("ZB0", 15 - r, 143 - r), X(src, r, 256, 16)) for r in range(16)])
+
+    def place(ps, src, out):
+        tt(X("o1"), X(ps, 480, 496), X(src), A.add)
+        tt(X("o2"), X("o1"), X("trS"), A.min)
+        ts(X(out), X("o2"), 1536.0, A.add)
+
+    for t in range(4):
+        VL, z, E = "VL%d" % t, "z%d" % t, "E3%d" % (t % 2)
+        last = t == 3
+        if t > 0:
+            rec[VL] = [(0, 16, "R", "al%d" % t, n_in, True)]
+            rec[z] = [(0, 128, "R", "ay%d" % t, n_in, True), (128, 256, "R", "az%d" % t, n_in, True)]
+
+        expand(scp, "zE", z, 0, 128)
+        tt(X("dz"), ind_x(X(VL)), X(z), A.subtract)
+        ts(X("nn"), X("dz"), 1.0, A.is_gt)
+        ts(X("nm"), X("dz"), -1.0, A.is_lt)
+        mms([(X("ps0", 0, 256), X("VW"), X("nn")), (X("ps0", 0, 256), X("VW"), X("nm"))])
+        if t > 0:
+            place("ps2", "o3", "offR")
+        ts(X("Pb"), X("ps0", 0, 256), pc(20), A.is_lt)
+        mms([(X("ps1", 0, 256), X("M2"), X("Pb"))])
+        mms([(X("ps1", 256, 512), X("M1"), X("Pb"))])
+        mms([(X("ps0", 256, 512), X("ALT"), X("Pb"))])
+        scp(X("m2"), X("ps1", 0, 256))
+        ts(X("vS"), X(VL), -1536.0, A.add)
+        if t == 0:
+            for j in range(4):
+                a, b = j * C4, (j + 1) * C4
+                ts(X("nbS", a, b), X("nbI", a, b), -1536.0, A.add)
+                if j == 1:
+                    consts_b()
+        else:
+            cp(IND(X("nbS", 0, WT), X("offR")), X("wv"))
+        ts(X("conU"), ind_n(X(VL)), 1536.0, A.add)
+        expand(cp, "maskE", "m2", 0, 64)
+        for c in range(1, 4):
+            expand(scp, "maskE", "m2", 64 * c, 64 * c + 64)
+            if c == 1:
+                act(X("conF"), ind_n(X(VL)), F.Copy)
+        scp(X("ohb"), X("ps1", 256, 512))
+
+        def gather_nb(c):
+            s = 1024 * c
+            tt(X("mk", s, s + 1024), ind_n(X("conU", 64 * c, 64 * c + 64)), X("maskE", s, s + 1024), A.mult)
+            for par, zz in ((0, "ZFe"), (1, "ZFo")):
+                col = par * 128 + (c % 2) * 64
+                mms([(X("ps%d" % (3 + c // 2), col, col + 64), X(zz, 15 - k, 143 - k), X("mk", s + k, s + 1024, 16))
+                     for k in range(16)])
+
+        def lists(h):
+            ts(X("cU", 256 * h, 256 * h + 256), X("ps%d" % (3 + h), 0, 256), 1536.0, A.add)
+
+        gather_nb(0)
+        gather_nb(1)
+        tt(X("co"), X("ps1", 256, 512), X("conF"), A.mult)
+        if t == 0:
+            consts_c()
+        mms([(X("ps2", 0, 16), X("ZFa", 15 - r, 143 - r), X("co", r, 256, 16)) for r in range(16)])
+        act(X("ps0", 0, 256), X("ps0", 256, 512), F.Identity, bias=1.0, scale=-(1.0 - 2.0 ** -16))
+        act(X("ps0", 256, 512), X("ps0", 256, 512), F.Identity, bias=2.0 ** -16, scale=1.0 - 2.0 ** -16)
+        gather_nb(2)
+        lists(0)
+        ts(X("TLu"), X("ps2", 0, 16), 1536.0, A.add)
+        gather_nb(3)
+        expand(scp, "zE", z, 128, 256)
+        ts(X("W0"), X("Pb"), pc(12), A.mult, pc(11), A.add)
+        for h in range(2):
+            for par in range(2):
+                a = 256 * par + 128 * h
+                tt(X("Wt", 256 * h + 128 * par, 256 * h + 128 * par + 128), X("ps0", a, a + 128), X("W0", 128 * h, 128 * h + 128), A.mult)
+
+        def dsum(c, par):
+            s = 1024 * (2 * c + par)
+            col = par * 128 + (c % 2) * 64
+            mms([(X("ps%d" % (5 + c // 2), col, col + 64), X("ZZ", 15 - k, 143 - k), X("dd", s + k, s + 1024, 16)) for k in range(16)])
+
+        def ccols(c, par):
+            col = 256 * (c // 2) + par * 128 + (c % 2) * 64
+            return X("cU", col, col + 64)
+
+        def raw(c):
+            act(X("xg", 1024 * c, 1024 * c + 1024), ind_x(ccols(c, 1)), F.Copy)
+
+        def raw_sub(c):
+            for b in range(2):
+                a0 = 1024 * c + 512 * b
+                mms([(X("ps%d" % b), X("D0"), X("xg", a0, a0 + 512)), (X("ps%d" % b), X("In"), X("zE", a0, a0 + 512))])
+
+        def raw_abs(c):
+            s = 1024 * (2 * c + 1)
+            for b in range(2):
+                act(X("dd", s + 512 * b, s + 512 * b + 512), X("ps%d" % b), F.Abs)
+            dsum(c, 1)
+
+        def cand(c, par):
+            s = 1024 * (2 * c + par)
+            tt(X("dd", s, s + 1024), ind_x(ccols(c, par)), X("zE", 1024 * c, 1024 * c + 1024), A.subtract)
+            act(X("dd", s, s + 1024), X("dd", s, s + 1024), F.Abs)
+            dsum(c, par)
+
+        def pairs():
+            cp(X("VB"), IND(X("idW"), X(VL)))
+            for q in range(16):
+                ts(erow(E, q), X("VB", 16 * q, 256), X("vS", q, q + 1), A.is_equal)
+            diag = (T[E][:, :, 0:16], E, 0, 4096)
+            tt(diag, diag, (T.TRI[:, :, :], "TRI", 0, 256), A.mult)
+
+        raw(0)
+        raw_sub(0)
+        raw(1)
+        cand(0, 0)
+        raw_abs(0)
+        raw_sub(1)
+        lists(1)
+        pairs()
+        if not last:
+            count("ps2", lambda q: X("BLKb"), E)
+        raw(2)
+        tt(X("d0"), ind_x(X("TLu")), X(z), A.subtract)
+        act(X("d0"), X("d0"), F.Abs)
+        mms([(X("ps7", 256, 512), X("BLKb"), X("d0"))])
+        act(X("adz"), X("dz"), F.Abs)
+        raw_abs(1)
+        raw_sub(2)
+        cand(1, 0)
+        if not last:
+            scp(X("cb"), X("ps2", 0, 256))
+            to_list("ps2", "cb")
+        tt(X("dlt"), X("adz"), X(z), A.subtract)
+        if not last:
+            ts(X("xi"), X("dz"), 0.5, A.mult, -0.25, A.add)
+            tt(X("xn"), X("xi"), X(z), A.add)
+        cand(2, 0)
+        raw_abs(2)
+        ts(X("hb2"), X("ps7", 256, 512), X("Hc", t, t + 1), A.is_lt, 2.0, A.mult)
+        tt(X("hc"), X("hb2"), X("co"), A.mult)
+        if not last:
+            act(X("junk"), X("hb2"), F.Copy, acc=X("hs", t, t + 1))
+        cand(3, 0)
+
+        def relu(h):
+            act(X("ps%d" % (5 + h), 0, 256), X("ps%d" % (5 + h), 0, 256), F.Relu, bias=X("bB"), scale=-2.0)
+
+        def tail_a(h):
+            tt(X("hw", 256 * h, 256 * h + 256), X("ps%d" % (5 + h), 0, 256), X("Wt", 256 * h, 256 * h + 256), A.min)
+            s = X("ps7", 128 * h, 128 * h + 128)
+            mms([(s, X("B7"), X("hw", 256 * h, 256 * h + 128)), (s, X("B7"), X("hw", 256 * h + 128, 256 * h + 256)),
+                 (s, X("Ih"), X("hb2", 128 * h, 128 * h + 128))])
+
+        def tail_b(h):
+            a, b = 128 * h, 128 * h + 128
+            s = X("ps7", a, b)
+            for par in range(2):
+                u = 256 * h + 128 * par
+                tt(X("fi", u, u + 128), X("hw", u, u + 128), s, A.is_gt)
+            tt(X("fc", 256 * h, 256 * h + 256), X("ps%d" % (3 + h), 0, 256), X("fi", 256 * h, 256 * h + 256), A.mult)
+            lo = X("ps1", 256 + a, 256 + b)
+            ts(lo, s, 0.0, A.is_equal)
+            tt(X("lc", a, b), lo, X("conF", a, b), A.mult)
+            o = X("ps0", a, b)
+            mms([(o, X("BFh"), X("hc", a, b)), (o, X("BF1"), X("fc", 256 * h, 256 * h + 128)),
+                 (o, X("BF1"), X("fc", 256 * h + 128, 256 * h + 256)), (o, X("BF15"), X("lc", a, b))])
+            tt(lo, lo, X("dlt", a, b), A.mult)
+            zn = X("zn%d" % t, a, b)
+            tt(zn, lo, X(z, a, b), A.add)
+            if not last:
+                send(T["z%d" % (t + 1)][:, a:b], zn, ("ay%d" if h == 0 else "az%d") % (t + 1), m_lo)
+            else:
+                dma("Y", T.yz[:, a:b], [], zn[0], [zn], "yz%d" % h)
+            tt(X("pk", 256 + a, 256 + b), s, X("hb2", a, b), A.is_gt)
+            cp(X("pk", a, b), o)
+
+        def weigh(qs, on_scalar):
+            for q in qs:
+                if on_scalar:
+                    act(X("LQ", 128 * q, 128 * q + 128), X("BLKb"), F.Copy, scale=X("rp", q, q + 1))
+                else:
+                    ts(X("LQ", 128 * q, 128 * q + 128), X("BLKb"), X("rp", q, q + 1), A.mult)
+
+        relu(0)
+        cand(3, 1)
+        relu(1)
+        tail_a(0)
+        tail_b(0)
+        if not last:
+            place("ps2", "vS", "offA")
+            cp(IND(X("xdS", 0, WT), X("offA")), X("xn"))
+        tail_a(1)
+        tail_b(1)
+        mms([(X("ps5", 256, 288), X("ZF0", 15 - r, 143 - r), X("pk", r, 512, 16)) for r in range(16)])
+        ts(X("VN%d" % t if not last else "yvS"), X("ps5", 256, 272), 1536.0, A.add)
+        if not last:
+            send(T["VL%d" % (t + 1)][:, :], X("VN%d" % t), "al%d" % (t + 1), m_hi)
+        else:
+            dma("Y", T.yv[:, :], [], T.yvS[:, :], [X("yvS")], "yv")
+        scp(X("rp"), X("ps5", 272, 288))
+        weigh(range(0, 10), False)
+        weigh(range(10, 16), True)
+        count("ps2", lambda q: X("LQ", 128 * q, 128 * q + 128), E)
+        nw = X("ps0", 0, 256)
+        tt(nw, nw, X("conF"), A.subtract)
+        tt(nw, nw, X("ohb"), A.mult)
+        tt(X("wv"), nw, X("conF"), A.add)
+        ts(X("q1"), X("rp"), -4096.0, A.mult, 4096.0, A.add)
+        tt(X("o3"), X("q1"), X("vS"), A.add)
+        scp(X("crb"), X("ps2", 0, 256))
+        to_list("ps2", "crb")
+        if not last:
+            cp(X("hsb", t, t + 1), X("hs", t, t + 1))
+            mms([(X("ps7", 256, 257), X("AW"), X("hsb", t, t + 1))])
+            ts(X("hi0", t, t + 1), X("ps7", 256, 257), -1.0, A.mult, 2048.0, A.add)
+            ts(X("hi1", t, t + 1), X("hi0", t, t + 1), 15, A.bitwise_and)
+            tt(X("Hc", t + 1, t + 2), X("hi1", t, t + 1), X("thF", 0, 1), A.add)
+    place("ps2", "o3", "offR")
+    cp(IND(X("nbS", 0, WT), X("offR")), X("wv"))
+
+    for j in range(4):
+        a, b = j * C4, (j + 1) * C4
+        if j % 2 == 0:
+            ts(X("yn", a, b), X("nbS", a, b), 1536.0, A.add)
+        else:
+            act(X("yn", a, b), X("nbS", a, b), F.Copy, bias=1536.0)
+        dma("Y", T.ynb[:, a:b], [], T.yn[:, a:b], [X("yn", a, b)], "y%d" % j)
+    fin = {s: cnt[s] for s in cnt}
+    for d in DMAS:
+        fin["d_" + d] = 16
+    fin["loc"] = loc[0]
+    for s in fin:
+        if known["G"].get(s, 0) < fin[s]:
+            g.wait_ge(T.sem[s], fin[s])

@@ -14,10 +14,10 @@ SCRATCH = {
 
 def _decl():
     for names, cols, d in (("maskE zE xg", 4096, "bfloat16"), ("mk", 4096, "float16"), ("dd", 8192, "bfloat16"), ("LQ", 2048, "bfloat16"),
-                           ("dz adz nn nm Pb m2 ohb dlt d0 hb2 junk W0 cb crb xn", 256, "bfloat16"), ("Wt hw fi", 512, "bfloat16"),
+                           ("dz adz nn nm Pb m2 ohb dlt d0 hb2 junk W0 cb crb xi xn", 256, "bfloat16"), ("Wt hw fi", 512, "bfloat16"),
                            ("VB co hc lc", 256, "float16"), ("fc pk", 512, "float16"), ("conF wv rr", 256, "float32"),
                            ("conU", 256, "uint16"), ("cU", 512, "uint16"), ("TLu offA offR", 16, "uint16"),
-                           ("vS rp q1 o1 o2 o3 yvS tr trS", 16, "float32"), ("pvI", 16, "int32"), ("xi", 256, "int32"),
+                           ("vS rp q1 o1 o2 o3 yvS tr trS", 16, "float32"), ("pvI", 16, "int32"),
                            ("thI", 2, "int32"), ("thF", 2, "float32"), ("bB", 1, "float32"), ("Hc hs", 4, "float32"),
                            ("hsb", 4, "bfloat16"), ("hi0 hi1", 4, "int32"), ("pI pB", 8, "int32"), ("pC", 32, "float32"),
                            ("ones ZZ ta tb ZB0", 144, "bfloat16"), ("ZFe ZFo ZFa ZF0", 144, "float16"),
@@ -219,6 +219,7 @@ def rank_program(g, core, T, topo):
         ts(X(n), X("BLKb"), pc(j), A.mult)
     for n, b in (("D0", 0), ("D2", 2), ("CA", -15), ("CB", -14), ("D1", 1)):
         sel(X(n), X("BLKb"), [[-1, 128]], A.is_equal, b, 1)
+    ts(X("In"), X("D0"), -1.0, A.mult)
     ts(X("D0n"), X("D0"), pc(23), A.mult)
     tt(X("mt"), X("CA"), X("D0n"), A.subtract)
     tt(X("M2a"), X("D2"), X("CB"), A.add)
@@ -241,7 +242,6 @@ def rank_program(g, core, T, topo):
     def consts_c():
         ts(X("ZF0"), X("ZZ"), pc(25), A.mult)
         ts(X("ZB0"), X("ZZ"), pc(26), A.mult)
-        ts(X("In"), X("D0"), -1.0, A.mult)
         ts(X("Ih"), X("D0"), 0.5, A.mult)
         ts(X("B7"), X("BLKb"), 0.4375, A.mult)
         cp(X("BF1"), X("BLKb"))
@@ -257,22 +257,29 @@ def rank_program(g, core, T, topo):
     adr = topo.addr(nxt)
     eng = topo.engines(core, nxt)
     half = len(eng) // 2
-    m_lo, m_hi = sum(1 << e for e in eng[:half]), sum(1 << e for e in eng[half:])
+    msk = sum(1 << e for e in eng[:half])
     n_in = len(topo.engines(prv, core)) // 2
     loc = [0]
 
-    def send(dst, src, sem, m):
+    def send(dst, src, sem):
         deps = {}
         need("G", src[1], src[2], src[3], False, deps)
         waits("G", deps)
-        g.remote_dma(dst, src[0], T.sem[sem], T.sem.loc, adr[1], adr[0], m)
+        g.remote_dma(dst, src[0], T.sem[sem], T.sem.loc, adr[1], adr[0], msk)
         loc[0] += half
+
+    def arrive(t):
+        rec["VL%d" % t] = [(0, 16, "R", "al%d" % t, n_in, True)]
+        rec["z%d" % t] = [(0, 128, "R", "ay%d" % t, n_in, True), (128, 256, "R", "az%d" % t, n_in, True)]
 
     def expand(copy, dst, src, i0, i1):
         a, b = 16 * i0, 16 * i1
         copy(X(dst, a, b, 16), X(src, i0, i1))
         for k in (8, 4, 2, 1):
             copy(X(dst, a + k, b, 2 * k), X(dst, a, b, 2 * k))
+
+    def targets(t, c):
+        expand(scp, "zE", "z%d" % t, 64 * c, 64 * c + 64)
 
     def ind_x(off):
         return IND(X("xdS", 0, W), off)
@@ -294,24 +301,38 @@ def rank_program(g, core, T, topo):
         tt(X("o2"), X("o1"), X("trS"), A.min)
         ts(X(out), X("o2"), 1536.0, A.add)
 
+    def new_contacts():
+        nw = X("ps0", 0, 256)
+        tt(nw, nw, X("conF"), A.subtract)
+        tt(nw, nw, X("ohb"), A.mult)
+        tt(X("wv"), nw, X("conF"), A.add)
+
     for t in range(4):
         VL, z, E = "VL%d" % t, "z%d" % t, "E3%d" % (t % 2)
         last = t == 3
-        if t > 0:
-            rec[VL] = [(0, 16, "R", "al%d" % t, n_in, True)]
-            rec[z] = [(0, 128, "R", "ay%d" % t, n_in, True), (128, 256, "R", "az%d" % t, n_in, True)]
 
-        expand(scp, "zE", z, 0, 128)
+        if t == 0:
+            targets(0, 0)
         tt(X("dz"), ind_x(X(VL)), X(z), A.subtract)
         ts(X("nn"), X("dz"), 1.0, A.is_gt)
         ts(X("nm"), X("dz"), -1.0, A.is_lt)
-        mms([(X("ps0", 0, 256), X("VW"), X("nn")), (X("ps0", 0, 256), X("VW"), X("nm"))])
+        mms([(X("ps6", 0, 256), X("VW"), X("nn")), (X("ps6", 0, 256), X("VW"), X("nm"))])
+        act(X("adz"), X("dz"), F.Abs)
+        mms([(X("ps5", 0, 256), X("D0"), X("adz")), (X("ps5", 0, 256), X("In"), X(z))])
+        if not last:
+            ts(X("xi"), X("dz"), 0.5, A.mult, 191.75, A.add)
+            mms([(X("ps5", 256, 512), X("D0"), X("xi")), (X("ps5", 256, 512), X("D0"), X(z))])
         if t > 0:
+            new_contacts()
             place("ps2", "o3", "offR")
-        ts(X("Pb"), X("ps0", 0, 256), pc(20), A.is_lt)
+        targets(t, 1)
+        scp(X("dlt"), X("ps5", 0, 256))
+        if not last:
+            act(X("xn"), X("ps5", 256, 512), F.Copy, bias=-192.0)
+        ts(X("Pb"), X("ps6", 0, 256), pc(20), A.is_lt)
         mms([(X("ps1", 0, 256), X("M2"), X("Pb"))])
         mms([(X("ps1", 256, 512), X("M1"), X("Pb"))])
-        mms([(X("ps0", 256, 512), X("ALT"), X("Pb"))])
+        mms([(X("ps6", 256, 512), X("ALT"), X("Pb"))])
         scp(X("m2"), X("ps1", 0, 256))
         ts(X("vS"), X(VL), -1536.0, A.add)
         if t == 0:
@@ -347,8 +368,8 @@ def rank_program(g, core, T, topo):
         if t == 0:
             consts_c()
         mms([(X("ps2", 0, 16), X("ZFa", 15 - r, 143 - r), X("co", r, 256, 16)) for r in range(16)])
-        act(X("ps0", 0, 256), X("ps0", 256, 512), F.Identity, bias=1.0, scale=-(1.0 - 2.0 ** -16))
-        act(X("ps0", 256, 512), X("ps0", 256, 512), F.Identity, bias=2.0 ** -16, scale=1.0 - 2.0 ** -16)
+        act(X("ps6", 0, 256), X("ps6", 256, 512), F.Identity, bias=1.0, scale=-(1.0 - 2.0 ** -16))
+        act(X("ps6", 256, 512), X("ps6", 256, 512), F.Identity, bias=2.0 ** -16, scale=1.0 - 2.0 ** -16)
         gather_nb(2)
         lists(0)
         ts(X("TLu"), X("ps2", 0, 16), 1536.0, A.add)
@@ -358,7 +379,7 @@ def rank_program(g, core, T, topo):
         for h in range(2):
             for par in range(2):
                 a = 256 * par + 128 * h
-                tt(X("Wt", 256 * h + 128 * par, 256 * h + 128 * par + 128), X("ps0", a, a + 128), X("W0", 128 * h, 128 * h + 128), A.mult)
+                tt(X("Wt", 256 * h + 128 * par, 256 * h + 128 * par + 128), X("ps6", a, a + 128), X("W0", 128 * h, 128 * h + 128), A.mult)
 
         def dsum(c, par):
             s = 1024 * (2 * c + par)
@@ -396,6 +417,9 @@ def rank_program(g, core, T, topo):
             diag = (T[E][:, :, 0:16], E, 0, 4096)
             tt(diag, diag, (T.TRI[:, :, :], "TRI", 0, 256), A.mult)
 
+        def relu(h):
+            act(X("ps%d" % (5 + h), 0, 256), X("ps%d" % (5 + h), 0, 256), F.Relu, bias=X("bB"), scale=-2.0)
+
         raw(0)
         raw_sub(0)
         raw(1)
@@ -410,27 +434,20 @@ def rank_program(g, core, T, topo):
         tt(X("d0"), ind_x(X("TLu")), X(z), A.subtract)
         act(X("d0"), X("d0"), F.Abs)
         mms([(X("ps7", 256, 512), X("BLKb"), X("d0"))])
-        act(X("adz"), X("dz"), F.Abs)
         raw_abs(1)
         raw_sub(2)
         cand(1, 0)
         if not last:
             scp(X("cb"), X("ps2", 0, 256))
             to_list("ps2", "cb")
-        tt(X("dlt"), X("adz"), X(z), A.subtract)
-        if not last:
-            ts(X("xi"), X("dz"), 0.5, A.mult, -0.25, A.add)
-            tt(X("xn"), X("xi"), X(z), A.add)
         cand(2, 0)
         raw_abs(2)
         ts(X("hb2"), X("ps7", 256, 512), X("Hc", t, t + 1), A.is_lt, 2.0, A.mult)
         tt(X("hc"), X("hb2"), X("co"), A.mult)
+        relu(0)
         if not last:
             act(X("junk"), X("hb2"), F.Copy, acc=X("hs", t, t + 1))
         cand(3, 0)
-
-        def relu(h):
-            act(X("ps%d" % (5 + h), 0, 256), X("ps%d" % (5 + h), 0, 256), F.Relu, bias=X("bB"), scale=-2.0)
 
         def tail_a(h):
             tt(X("hw", 256 * h, 256 * h + 256), X("ps%d" % (5 + h), 0, 256), X("Wt", 256 * h, 256 * h + 256), A.min)
@@ -455,11 +472,10 @@ def rank_program(g, core, T, topo):
             zn = X("zn%d" % t, a, b)
             tt(zn, lo, X(z, a, b), A.add)
             if not last:
-                send(T["z%d" % (t + 1)][:, a:b], zn, ("ay%d" if h == 0 else "az%d") % (t + 1), m_lo)
+                send(T["z%d" % (t + 1)][:, a:b], zn, ("ay%d" if h == 0 else "az%d") % (t + 1))
             else:
                 dma("Y", T.yz[:, a:b], [], zn[0], [zn], "yz%d" % h)
             tt(X("pk", 256 + a, 256 + b), s, X("hb2", a, b), A.is_gt)
-            cp(X("pk", a, b), o)
 
         def weigh(qs, on_scalar):
             for q in qs:
@@ -468,40 +484,41 @@ def rank_program(g, core, T, topo):
                 else:
                     ts(X("LQ", 128 * q, 128 * q + 128), X("BLKb"), X("rp", q, q + 1), A.mult)
 
-        relu(0)
+        tail_a(0)
         cand(3, 1)
         relu(1)
-        tail_a(0)
         tail_b(0)
         if not last:
             place("ps2", "vS", "offA")
-            cp(IND(X("xdS", 0, WT), X("offA")), X("xn"))
+            cp(X("hsb", t, t + 1), X("hs", t, t + 1))
+            mms([(X("ps4", 256, 257), X("AW"), X("hsb", t, t + 1))])
         tail_a(1)
+        cp(X("pk", 0, 128), X("ps0", 0, 128))
         tail_b(1)
+        cp(X("pk", 128, 256), X("ps0", 128, 256))
         mms([(X("ps5", 256, 288), X("ZF0", 15 - r, 143 - r), X("pk", r, 512, 16)) for r in range(16)])
+        if not last:
+            ts(X("hi0", t, t + 1), X("ps4", 256, 257), -1.0, A.mult, 2048.0, A.add)
+            ts(X("hi1", t, t + 1), X("hi0", t, t + 1), 15, A.bitwise_and)
+            tt(X("Hc", t + 1, t + 2), X("hi1", t, t + 1), X("thF", 0, 1), A.add)
         ts(X("VN%d" % t if not last else "yvS"), X("ps5", 256, 272), 1536.0, A.add)
         if not last:
-            send(T["VL%d" % (t + 1)][:, :], X("VN%d" % t), "al%d" % (t + 1), m_hi)
+            send(T["VL%d" % (t + 1)][:, :], X("VN%d" % t), "al%d" % (t + 1))
         else:
             dma("Y", T.yv[:, :], [], T.yvS[:, :], [X("yvS")], "yv")
         scp(X("rp"), X("ps5", 272, 288))
         weigh(range(0, 10), False)
         weigh(range(10, 16), True)
         count("ps2", lambda q: X("LQ", 128 * q, 128 * q + 128), E)
-        nw = X("ps0", 0, 256)
-        tt(nw, nw, X("conF"), A.subtract)
-        tt(nw, nw, X("ohb"), A.mult)
-        tt(X("wv"), nw, X("conF"), A.add)
+        if not last:
+            cp(IND(X("xdS", 0, WT), X("offA")), X("xn"))
+            arrive(t + 1)
+            targets(t + 1, 0)
         ts(X("q1"), X("rp"), -4096.0, A.mult, 4096.0, A.add)
         tt(X("o3"), X("q1"), X("vS"), A.add)
         scp(X("crb"), X("ps2", 0, 256))
         to_list("ps2", "crb")
-        if not last:
-            cp(X("hsb", t, t + 1), X("hs", t, t + 1))
-            mms([(X("ps7", 256, 257), X("AW"), X("hsb", t, t + 1))])
-            ts(X("hi0", t, t + 1), X("ps7", 256, 257), -1.0, A.mult, 2048.0, A.add)
-            ts(X("hi1", t, t + 1), X("hi0", t, t + 1), 15, A.bitwise_and)
-            tt(X("Hc", t + 1, t + 2), X("hi1", t, t + 1), X("thF", 0, 1), A.add)
+    new_contacts()
     place("ps2", "o3", "offR")
     cp(IND(X("nbS", 0, WT), X("offR")), X("wv"))
 

@@ -1,27 +1,28 @@
-import numpy as np
+import math
 from concourse.mybir import dt, AluOpType, AxisListType, ActivationFunctionType
 
 W = 3072
+LN2 = math.log(2.0)
 WT = W + 256
 
 SCRATCH = {
     "nbI": ("sbuf", [128, W], "int32"), "nbS": ("sbuf", [128, WT], "float32"), "xdS": ("sbuf", [128, WT], "bfloat16"),
-    "idW": ("sbuf", [128, W], "float32"), "yn": ("sbuf", [128, W], "float32"),
+    "idW": ("sbuf", [128, W], "float32"), "yn": ("sbuf", [128, WT], "float32"),
     "E30": ("sbuf", [128, 16, 256], "bfloat16"), "E31": ("sbuf", [128, 16, 256], "bfloat16"),
-    "TRI": ("sbuf", [128, 16, 16], "bfloat16"),
+    "Wt": ("sbuf", [128, 2, 256], "bfloat16"), "TRI": ("sbuf", [128, 16, 16], "bfloat16"),
 }
 
 
 def _decl():
     for names, cols, d in (("maskE zE xg", 4096, "bfloat16"), ("mk", 4096, "float16"), ("dd", 8192, "bfloat16"), ("LQ", 2048, "bfloat16"),
-                           ("dz adz nn nm Pb m2 ohb dlt d0 hb2 junk W0 cb crb xi xn", 256, "bfloat16"), ("Wt hw fi", 512, "bfloat16"),
-                           ("VB co hc lc", 256, "float16"), ("fc pk", 512, "float16"), ("conF wv rr", 256, "float32"),
+                           ("dz adz nn nm Pb m2 ohb dlt d0 hb2 cb crb xi xn", 256, "bfloat16"), ("hw fi", 512, "bfloat16"),
+                           ("VB0 VB1 VB2 VB3 co hc lc", 256, "float16"), ("fc pk0 pk1 pk2 pk3", 512, "float16"), ("conF wv rr", 256, "float32"),
                            ("conU", 256, "uint16"), ("cU", 512, "uint16"), ("TLu offA offR", 16, "uint16"),
                            ("vS rp q1 o1 o2 o3 yvS tr trS", 16, "float32"), ("pvI", 16, "int32"),
                            ("thI", 2, "int32"), ("thF", 2, "float32"), ("bB", 1, "float32"), ("Hc hs", 4, "float32"),
                            ("hsb", 4, "bfloat16"), ("hi0 hi1", 4, "int32"), ("pI pB", 8, "int32"), ("pC", 32, "float32"),
                            ("ones ZZ ta tb ZB0", 144, "bfloat16"), ("ZFe ZFo ZFa ZF0", 144, "float16"),
-                           ("BLKb D0 D1 D2 CA CB D0n mt M1 M2 M2a In Ih B7 AW VW ALT", 128, "bfloat16"),
+                           ("BLKb D0 D1 D2 CA CB D0n mt M1 M2 M2a In Ih B7 AW VW ALT KE KO", 128, "bfloat16"),
                            ("BF1 BFh BF15", 128, "float16"),
                            ("VL0 VL1 VL2 VL3 VN0 VN1 VN2 VN3", 16, "uint16"), ("z0 z1 z2 z3 zn0 zn1 zn2 zn3", 256, "bfloat16")):
         for n in names.split():
@@ -32,7 +33,7 @@ def _decl():
 
 _decl()
 DMAS = ["pv", "pz", "th", "xa", "xb", "n0", "n1", "n2", "n3", "y0", "y1", "y2", "y3", "yv", "yz0", "yz1"]
-SEMAPHORES = ["sV", "sS", "sP", "sG", "loc"] + ["d_" + d for d in DMAS] + ["a%s%d" % (n, t) for n in ("l", "y", "z") for t in range(4)]
+SEMAPHORES = ["sV", "sS", "sP", "sG", "loc"] + ["d_" + d for d in DMAS] + ["a%s%d" % (n, t) for n in ("l", "y", "z", "v") for t in range(4)]
 
 
 def rank_program(g, core, T, topo):
@@ -175,13 +176,13 @@ def rank_program(g, core, T, topo):
 
     C4, H2 = W // 4, W // 2
     dma("Y", T.pvI[:, :], [X("pvI")], T.pv[:, :], [], "pv")
+    dma("Y", T.thI[:, :], [X("thI")], T.th[:, :], [], "th")
     dma("S", T.z0[:, :], [X("z0")], T.pz[:, :], [], "pz")
     dma("Y", T.xdS[:, 0:H2], [X("xdS", 0, H2)], T.xd[:, 0:H2], [], "xa")
     dma("S", T.xdS[:, H2:W], [X("xdS", H2, W)], T.xd[:, H2:W], [], "xb")
     for j in range(4):
         a, b = j * C4, (j + 1) * C4
         dma("Y" if j % 2 == 0 else "S", T.nbI[:, a:b], [X("nbI", a, b)], T.nb[:, a:b], [], "n%d" % j)
-    dma("Y", T.thI[:, :], [X("thI")], T.th[:, :], [], "th")
 
     pc = lambda j: X("pC", j, j + 1)
     iota(X("pI", 0, 1), [[1, 1]], 0, 1)
@@ -208,8 +209,8 @@ def rank_program(g, core, T, topo):
     ts(pc(21), pc(1), -2.0, A.mult, 1.0, A.add)
     tt(pc(22), pc(21), pc(13), A.mult)
     ts(pc(23), pc(15), -1.0, A.mult, 1.0, A.add)
-    tt(pc(27), pc(11), pc(23), A.mult)
-    ts(pc(12), pc(27), 2.0 ** -16 - 1.0, A.mult)
+    ts(pc(28), pc(0), -LN2, A.mult)
+    ts(pc(29), pc(0), -LN2, A.mult, -16.0 * LN2, A.add)
     ts(pc(24), pc(1), -1.0, A.mult, 1.0, A.add)
     ts(pc(25), pc(0), 0.0, A.is_equal)
     ts(pc(26), pc(25), 4096.0, A.mult)
@@ -221,6 +222,8 @@ def rank_program(g, core, T, topo):
         sel(X(n), X("BLKb"), [[-1, 128]], A.is_equal, b, 1)
     ts(X("In"), X("D0"), -1.0, A.mult)
     ts(X("D0n"), X("D0"), pc(23), A.mult)
+    tt(X("KE"), X("D0n"), X("ALT"), A.add)
+    tt(X("KO"), X("D0n"), X("ALT"), A.subtract)
     tt(X("mt"), X("CA"), X("D0n"), A.subtract)
     tt(X("M2a"), X("D2"), X("CB"), A.add)
     tt(X("M2"), X("M2a"), X("mt"), A.add)
@@ -228,18 +231,16 @@ def rank_program(g, core, T, topo):
     sel(X("ta"), X("ones"), [[-16, 9], [0, 16]], A.is_ge, 0, 1)
     sel(X("tb"), X("ta"), [[16, 9], [0, 16]], A.is_ge, 15, -1)
     sel(X("ZZ"), X("tb"), [[0, 9], [1, 16]], A.is_equal, -15, 0)
-    iota(X("idW"), [[1, W]], -1536, 0)
     iota(X("rr"), [[0, 16], [1, 16]], 0, 0)
     iota(X("tr"), [[16, 16]], W - 1536, 0)
+    iota(X("idW"), [[1, W]], -1536, 0)
     cp(X("VL0"), X("pvI"))
 
-    def consts_b():
+    def more_consts():
         ts(X("ZFe"), X("ZZ"), pc(24), A.mult)
         ts(X("ZFo"), X("ZZ"), pc(1), A.mult)
         cp(X("ZFa"), X("ZZ"))
         ts((T.TRI[:, :, :], "TRI", 0, 256), X("rr"), pc(0), A.is_gt)
-
-    def consts_c():
         ts(X("ZF0"), X("ZZ"), pc(25), A.mult)
         ts(X("ZB0"), X("ZZ"), pc(26), A.mult)
         ts(X("Ih"), X("D0"), 0.5, A.mult)
@@ -270,6 +271,7 @@ def rank_program(g, core, T, topo):
 
     def arrive(t):
         rec["VL%d" % t] = [(0, 16, "R", "al%d" % t, n_in, True)]
+        rec["VB%d" % t] = [(0, 256, "R", "av%d" % t, n_in, True)]
         rec["z%d" % t] = [(0, 128, "R", "ay%d" % t, n_in, True), (128, 256, "R", "az%d" % t, n_in, True)]
 
     def expand(copy, dst, src, i0, i1):
@@ -308,7 +310,7 @@ def rank_program(g, core, T, topo):
         tt(X("wv"), nw, X("conF"), A.add)
 
     for t in range(4):
-        VL, z, E = "VL%d" % t, "z%d" % t, "E3%d" % (t % 2)
+        VL, VB, z, E, pk = "VL%d" % t, "VB%d" % t, "z%d" % t, "E3%d" % (t % 2), "pk%d" % t
         last = t == 3
 
         if t == 0:
@@ -325,22 +327,24 @@ def rank_program(g, core, T, topo):
         if t > 0:
             new_contacts()
             place("ps2", "o3", "offR")
-        targets(t, 1)
+        else:
+            targets(0, 1)
+        targets(t, 2)
         scp(X("dlt"), X("ps5", 0, 256))
         if not last:
             act(X("xn"), X("ps5", 256, 512), F.Copy, bias=-192.0)
         ts(X("Pb"), X("ps6", 0, 256), pc(20), A.is_lt)
         mms([(X("ps1", 0, 256), X("M2"), X("Pb"))])
         mms([(X("ps1", 256, 512), X("M1"), X("Pb"))])
-        mms([(X("ps6", 256, 512), X("ALT"), X("Pb"))])
+        mms([(X("ps6", 0, 256), X("KE"), X("Pb"))])
+        mms([(X("ps6", 256, 512), X("KO"), X("Pb"))])
         scp(X("m2"), X("ps1", 0, 256))
         ts(X("vS"), X(VL), -1536.0, A.add)
         if t == 0:
+            more_consts()
             for j in range(4):
                 a, b = j * C4, (j + 1) * C4
                 ts(X("nbS", a, b), X("nbI", a, b), -1536.0, A.add)
-                if j == 1:
-                    consts_b()
         else:
             cp(IND(X("nbS", 0, WT), X("offR")), X("wv"))
         ts(X("conU"), ind_n(X(VL)), 1536.0, A.add)
@@ -349,7 +353,6 @@ def rank_program(g, core, T, topo):
             expand(scp, "maskE", "m2", 64 * c, 64 * c + 64)
             if c == 1:
                 act(X("conF"), ind_n(X(VL)), F.Copy)
-        scp(X("ohb"), X("ps1", 256, 512))
 
         def gather_nb(c):
             s = 1024 * c
@@ -365,21 +368,16 @@ def rank_program(g, core, T, topo):
         gather_nb(0)
         gather_nb(1)
         tt(X("co"), X("ps1", 256, 512), X("conF"), A.mult)
-        if t == 0:
-            consts_c()
+        cp(X("ohb"), X("ps1", 256, 512))
         mms([(X("ps2", 0, 16), X("ZFa", 15 - r, 143 - r), X("co", r, 256, 16)) for r in range(16)])
-        act(X("ps6", 0, 256), X("ps6", 256, 512), F.Identity, bias=1.0, scale=-(1.0 - 2.0 ** -16))
-        act(X("ps6", 256, 512), X("ps6", 256, 512), F.Identity, bias=2.0 ** -16, scale=1.0 - 2.0 ** -16)
+        for par in range(2):
+            act((T.Wt[:, :, 128 * par:128 * par + 128], "Wt", 0, 512), X("ps6", 256 * par, 256 * par + 256), F.Exp,
+                bias=pc(28 + par), scale=-16.0 * LN2)
         gather_nb(2)
         lists(0)
         ts(X("TLu"), X("ps2", 0, 16), 1536.0, A.add)
         gather_nb(3)
-        expand(scp, "zE", z, 128, 256)
-        ts(X("W0"), X("Pb"), pc(12), A.mult, pc(11), A.add)
-        for h in range(2):
-            for par in range(2):
-                a = 256 * par + 128 * h
-                tt(X("Wt", 256 * h + 128 * par, 256 * h + 128 * par + 128), X("ps6", a, a + 128), X("W0", 128 * h, 128 * h + 128), A.mult)
+        targets(t, 3)
 
         def dsum(c, par):
             s = 1024 * (2 * c + par)
@@ -411,9 +409,10 @@ def rank_program(g, core, T, topo):
             dsum(c, par)
 
         def pairs():
-            cp(X("VB"), IND(X("idW"), X(VL)))
+            if t == 0:
+                cp(X(VB), IND(X("idW"), X(VL)))
             for q in range(16):
-                ts(erow(E, q), X("VB", 16 * q, 256), X("vS", q, q + 1), A.is_equal)
+                ts(erow(E, q), X(VB, 16 * q, 256), X("vS", q, q + 1), A.is_equal)
             diag = (T[E][:, :, 0:16], E, 0, 4096)
             tt(diag, diag, (T.TRI[:, :, :], "TRI", 0, 256), A.mult)
 
@@ -442,15 +441,15 @@ def rank_program(g, core, T, topo):
             to_list("ps2", "cb")
         cand(2, 0)
         raw_abs(2)
-        ts(X("hb2"), X("ps7", 256, 512), X("Hc", t, t + 1), A.is_lt, 2.0, A.mult)
-        tt(X("hc"), X("hb2"), X("co"), A.mult)
+        hb = X("ps7", 256, 512)
+        ts(hb, hb, X("Hc", t, t + 1), A.is_lt, 2.0, A.mult)
+        tt(X("hc"), hb, X("co"), A.mult)
         relu(0)
-        if not last:
-            act(X("junk"), X("hb2"), F.Copy, acc=X("hs", t, t + 1))
+        act(X("hb2"), hb, F.Copy, acc=X("hs", t, t + 1))
         cand(3, 0)
 
         def tail_a(h):
-            tt(X("hw", 256 * h, 256 * h + 256), X("ps%d" % (5 + h), 0, 256), X("Wt", 256 * h, 256 * h + 256), A.min)
+            tt(X("hw", 256 * h, 256 * h + 256), X("ps%d" % (5 + h), 0, 256), (T.Wt[:, h, :], "Wt", 256 * h, 256 * h + 256), A.min)
             s = X("ps7", 128 * h, 128 * h + 128)
             mms([(s, X("B7"), X("hw", 256 * h, 256 * h + 128)), (s, X("B7"), X("hw", 256 * h + 128, 256 * h + 256)),
                  (s, X("Ih"), X("hb2", 128 * h, 128 * h + 128))])
@@ -475,7 +474,7 @@ def rank_program(g, core, T, topo):
                 send(T["z%d" % (t + 1)][:, a:b], zn, ("ay%d" if h == 0 else "az%d") % (t + 1))
             else:
                 dma("Y", T.yz[:, a:b], [], zn[0], [zn], "yz%d" % h)
-            tt(X("pk", 256 + a, 256 + b), s, X("hb2", a, b), A.is_gt)
+            tt(X(pk, 256 + a, 256 + b), s, X("hb2", a, b), A.is_gt)
 
         def weigh(qs, on_scalar):
             for q in qs:
@@ -487,16 +486,18 @@ def rank_program(g, core, T, topo):
         tail_a(0)
         cand(3, 1)
         relu(1)
+        if last:
+            act(X("yn", 0, W), X("nbS", 0, W), F.Copy, bias=1536.0)
         tail_b(0)
         if not last:
             place("ps2", "vS", "offA")
-            cp(X("hsb", t, t + 1), X("hs", t, t + 1))
+            scp(X("hsb", t, t + 1), X("hs", t, t + 1))
             mms([(X("ps4", 256, 257), X("AW"), X("hsb", t, t + 1))])
         tail_a(1)
-        cp(X("pk", 0, 128), X("ps0", 0, 128))
+        cp(X(pk, 0, 128), X("ps0", 0, 128))
         tail_b(1)
-        cp(X("pk", 128, 256), X("ps0", 128, 256))
-        mms([(X("ps5", 256, 288), X("ZF0", 15 - r, 143 - r), X("pk", r, 512, 16)) for r in range(16)])
+        cp(X(pk, 128, 256), X("ps0", 128, 256))
+        mms([(X("ps5", 256, 288), X("ZF0", 15 - r, 143 - r), X(pk, r, 512, 16)) for r in range(16)])
         if not last:
             ts(X("hi0", t, t + 1), X("ps4", 256, 257), -1.0, A.mult, 2048.0, A.add)
             ts(X("hi1", t, t + 1), X("hi0", t, t + 1), 15, A.bitwise_and)
@@ -504,6 +505,9 @@ def rank_program(g, core, T, topo):
         ts(X("VN%d" % t if not last else "yvS"), X("ps5", 256, 272), 1536.0, A.add)
         if not last:
             send(T["VL%d" % (t + 1)][:, :], X("VN%d" % t), "al%d" % (t + 1))
+            send(T["VB%d" % (t + 1)][:, :], X(pk, 0, 256), "av%d" % (t + 1))
+            arrive(t + 1)
+            targets(t + 1, 0)
         else:
             dma("Y", T.yv[:, :], [], T.yvS[:, :], [X("yvS")], "yv")
         scp(X("rp"), X("ps5", 272, 288))
@@ -512,23 +516,19 @@ def rank_program(g, core, T, topo):
         count("ps2", lambda q: X("LQ", 128 * q, 128 * q + 128), E)
         if not last:
             cp(IND(X("xdS", 0, WT), X("offA")), X("xn"))
-            arrive(t + 1)
-            targets(t + 1, 0)
+            targets(t + 1, 1)
         ts(X("q1"), X("rp"), -4096.0, A.mult, 4096.0, A.add)
         tt(X("o3"), X("q1"), X("vS"), A.add)
         scp(X("crb"), X("ps2", 0, 256))
         to_list("ps2", "crb")
     new_contacts()
     place("ps2", "o3", "offR")
-    cp(IND(X("nbS", 0, WT), X("offR")), X("wv"))
+    ot = IND(X("yn", 0, WT), X("offR"))
+    op("V", lambda e: e.tensor_scalar(ot[0], T.wv[:, :], 1.0, 1536.0, A.mult, A.add), [X("wv"), ot[2]], [ot[1]])
 
     for j in range(4):
         a, b = j * C4, (j + 1) * C4
-        if j % 2 == 0:
-            ts(X("yn", a, b), X("nbS", a, b), 1536.0, A.add)
-        else:
-            act(X("yn", a, b), X("nbS", a, b), F.Copy, bias=1536.0)
-        dma("Y", T.ynb[:, a:b], [], T.yn[:, a:b], [X("yn", a, b)], "y%d" % j)
+        dma("Y" if j % 2 == 0 else "S", T.ynb[:, a:b], [], T.yn[:, a:b], [X("yn", a, b)], "y%d" % j)
     fin = {s: cnt[s] for s in cnt}
     for d in DMAS:
         fin["d_" + d] = 16

import math
from concourse.mybir import dt, AluOpType, AxisListType, ActivationFunctionType

W = 3072
LN2 = math.log(2.0)
WT = W + 256

SCRATCH = {
    "nbI": ("sbuf", [128, W], "int32"), "nbS": ("sbuf", [128, WT], "float32"), "xdS": ("sbuf", [128, WT], "bfloat16"),
    "idW": ("sbuf", [128, W], "float32"), "yn": ("sbuf", [128, WT], "float32"),
    "E30": ("sbuf", [128, 16, 256], "bfloat16"), "E31": ("sbuf", [128, 16, 256], "bfloat16"),
    "Wt": ("sbuf", [128, 2, 256], "bfloat16"), "TRI": ("sbuf", [128, 16, 16], "bfloat16"),
}


def _decl():
    for names, cols, d in (("maskE zE xg", 4096, "bfloat16"), ("mk", 4096, "float16"), ("dd", 8192, "bfloat16"), ("LQ", 2048, "bfloat16"),
                           ("dz adz nn nm Pb m2 ohb dlt d0 hb2 cb crb xi xn", 256, "bfloat16"), ("hw fi", 512, "bfloat16"),
                           ("VB0 VB1 VB2 VB3 co hc lc", 256, "float16"), ("fc pk0 pk1 pk2 pk3", 512, "float16"), ("conF wv rr", 256, "float32"),
                           ("conU", 256, "uint16"), ("cU", 512, "uint16"), ("TLu offA offR", 16, "uint16"),
                           ("vS rp q1 o1 o2 o3 yvS tr trS", 16, "float32"), ("pvI", 16, "int32"),
                           ("thI", 2, "int32"), ("thF", 2, "float32"), ("bB", 1, "float32"), ("Hc hs", 4, "float32"),
                           ("hsb", 4, "bfloat16"), ("hi0 hi1", 4, "int32"), ("pI pB", 8, "int32"), ("pC", 32, "float32"),
                           ("ones ZZ ta tb ZB0", 144, "bfloat16"), ("ZFe ZFo ZFa ZF0", 144, "float16"),
                           ("BLKb D0 D1 D2 CA CB D0n mt M1 M2 M2a In Ih B7 AW VW ALT KE KO", 128, "bfloat16"),
                           ("BF1 BFh BF15", 128, "float16"),
                           ("VL0 VL1 VL2 VL3 VN0 VN1 VN2 VN3", 16, "uint16"), ("z0 z1 z2 z3 zn0 zn1 zn2 zn3", 256, "bfloat16")):
        for n in names.split():
            SCRATCH[n] = ("sbuf", [128, cols], d)
    for b in range(8):
        SCRATCH["ps%d" % b] = ("psum", [128, 512], "float32")


_decl()
DMAS = ["pv", "pz", "th", "xa", "xb", "n0", "n1", "n2", "n3", "y0", "y1", "y2", "y3", "yv", "yz0", "yz1"]
SEMAPHORES = ["sV", "sS", "sP", "sG", "loc"] + ["d_" + d for d in DMAS] + ["a%s%d" % (n, t) for n in ("l", "y", "z", "v") for t in range(4)]


def rank_program(g, core, T, topo):
    rank = T.rank_of(core)
    if rank is None:
        return
    A, F = AluOpType, ActivationFunctionType
    ENG = {"V": g.vector, "S": g.scalar, "P": g.tensor, "G": g, "Y": g.sync}
    cnt = {"sV": 0, "sS": 0, "sP": 0, "sG": 0}
    known = {q: {} for q in ENG}
    snap = {}
    rec = {}

    def need(q, name, lo, hi, wr, out):
        ps = name[:2] == "ps"
        for (a, b, q2, s, c, w2) in rec.get(name, ()):
            if (ps and q2 != q) or (a < hi and lo < b and (wr or w2)):
                if out.get(s, 0) < c:
                    out[s] = c

    def note(q, name, lo, hi, s, c, wr):
        keep = []
        for x in rec.get(name, []):
            inside = lo <= x[0] and x[1] <= hi
            if inside and (wr or (x[2] == q and not x[5] and x[3] == s)):
                continue
            keep.append(x)
        keep.append((lo, hi, q, s, c, wr))
        rec[name] = keep

    def waits(q, deps):
        k = known[q]
        for s in sorted(deps, key=lambda s: -len(snap.get((s, deps[s]), ()))):
            c = deps[s]
            if k.get(s, 0) >= c:
                continue
            ENG[q].wait_ge(T.sem[s], c)
            for s2, c2 in snap.get((s, c), {}).items():
                if k.get(s2, 0) < c2:
                    k[s2] = c2
            k[s] = max(k.get(s, 0), c)

    def op(q, emit, reads, writes, sem=None, inc=1):
        deps = {}
        for x in reads:
            need(q, x[1], x[2], x[3], False, deps)
        for x in writes:
            need(q, x[1], x[2], x[3], True, deps)
        waits(q, deps)
        r = emit(ENG[q])
        if sem is None:
            s = "s" + q
            cnt[s] += 1
            c = cnt[s]
        else:
            s, c = sem, inc
        r.then_inc(T.sem[s], inc)
        snap[(s, c)] = dict(known[q])
        for x in reads:
            note(q, x[1], x[2], x[3], s, c, False)
        for x in writes:
            note(q, x[1], x[2], x[3], s, c, True)

    def X(n, a=0, b=None, st=1):
        if b is None:
            b = SCRATCH[n][1][1]
        return (T[n][:, a:b:st] if st > 1 else T[n][:, a:b], n, a, b)

    def IND(win, off):
        return (win[0].indirect(off[0]), win, off)

    def rd(x):
        return [x[1], x[2]] if len(x) == 3 else [x]

    def tt(out, a, b, o):
        op("V", lambda e: e.tensor_tensor(out[0], a[0], b[0], o), rd(a) + rd(b), [out])

    def ts(out, a, s1, o0, s2=None, o1=None):
        reads = rd(a)
        v1, v2 = s1, s2
        if isinstance(s1, tuple):
            reads = reads + [s1]; v1 = s1[0]
        if isinstance(s2, tuple):
            reads = reads + [s2]; v2 = s2[0]
        if o1 is None:
            op("V", lambda e: e.tensor_scalar(out[0], a[0], v1, None, o0), reads, [out])
        else:
            op("V", lambda e: e.tensor_scalar(out[0], a[0], v1, v2, o0, o1), reads, [out])

    def cp(out, a):
        if len(out) == 3:
            op("V", lambda e: e.tensor_copy(out[0], a[0]), rd(a) + [out[2]], [out[1]])
        else:
            op("V", lambda e: e.tensor_copy(out[0], a[0]), rd(a), [out])

    def act(out, a, f, bias=None, scale=None, acc=None):
        kw = {}
        reads, writes = rd(a), [out]
        for nm, v in (("bias", bias), ("scale", scale)):
            if v is not None:
                if isinstance(v, tuple):
                    reads = reads + [v]; kw[nm] = v[0]
                else:
                    kw[nm] = v
        if acc is not None:
            writes = writes + [acc]; kw["accum_out"] = acc[0]
        op("S", lambda e: e.activation(out[0], a[0], f, **kw), reads, writes)

    def scp(out, a):
        act(out, a, F.Copy)

    def mms(items):
        deps = {}
        for (o, l, r) in items:
            need("P", o[1], o[2], o[3], True, deps)
            need("P", l[1], l[2], l[3], False, deps)
            need("P", r[1], r[2], r[3], False, deps)
        waits("P", deps)
        n = len(items)
        for j, (o, l, r) in enumerate(items):
            g.tensor.matmul(o[0], l[0], r[0], j == 0, j == n - 1).then_inc(T.sem.sP, 1)
        cnt["sP"] += n
        c = cnt["sP"]
        snap[("sP", c)] = dict(known["P"])
        for (o, l, r) in items:
            note("P", l[1], l[2], l[3], "sP", c, False)
            note("P", r[1], r[2], r[3], "sP", c, False)
        for (o, l, r) in items:
            note("P", o[1], o[2], o[3], "sP", c, True)

    def dma(q, out, oacc, in_, iacc, name):
        op(q, lambda e: e.dma_start(out, in_), iacc, oacc, sem="d_" + name, inc=16)

    def iota(x, pat, base, cm):
        kw = {} if SCRATCH[x[1]][2] == "int32" else {"allow_small_or_imprecise_dtypes": True}
        op("G", lambda e: e.iota(x[0], pat, base, cm, **kw), [], [x])

    def sel(out, a, pat, o, base, cm):
        op("G", lambda e: e.affine_select(out[0], a[0], pat, o, 0.0, base, cm), [a], [out])

    C4, H2 = W // 4, W // 2
    dma("Y", T.pvI[:, :], [X("pvI")], T.pv[:, :], [], "pv")
    dma("Y", T.thI[:, :], [X("thI")], T.th[:, :], [], "th")
    dma("S", T.z0[:, :], [X("z0")], T.pz[:, :], [], "pz")
    dma("Y", T.xdS[:, 0:H2], [X("xdS", 0, H2)], T.xd[:, 0:H2], [], "xa")
    dma("S", T.xdS[:, H2:W], [X("xdS", H2, W)], T.xd[:, H2:W], [], "xb")
    for j in range(4):
        a, b = j * C4, (j + 1) * C4
        dma("Y" if j % 2 == 0 else "S", T.nbI[:, a:b], [X("nbI", a, b)], T.nb[:, a:b], [], "n%d" % j)

    pc = lambda j: X("pC", j, j + 1)
    iota(X("pI", 0, 1), [[1, 1]], 0, 1)
    op("V", lambda e: e.memset(T.ones[:, :], 1.0), [], [X("ones")])
    op("V", lambda e: e.memset(T.AW[:, :], 1.0 / 32), [], [X("AW")])
    ts(X("pI", 1, 2), X("pI", 0, 1), 15, A.bitwise_and)
    cp(pc(0), X("pI", 1, 2))
    for b in range(4):
        ts(X("pB", b, b + 1), X("pI", 1, 2), b, A.arith_shift_right, 1, A.bitwise_and)
    cp(X("pC", 1, 5), X("pB", 0, 4))
    for b in range(4):
        ts(pc(5 + b), pc(1 + b), 2.0 ** -(1 << b) - 1.0, A.mult, 1.0, A.add)
    tt(pc(9), pc(5), pc(6), A.mult)
    tt(pc(10), pc(7), pc(8), A.mult)
    tt(pc(11), pc(9), pc(10), A.mult)
    ts(pc(13), pc(0), 14.0, A.is_lt)
    ts(pc(14), pc(0), 14.0, A.is_equal)
    ts(pc(15), pc(0), 15.0, A.is_equal)
    ts(pc(16), pc(11), 32768.0, A.mult)
    tt(pc(17), pc(16), pc(13), A.mult)
    tt(pc(18), pc(17), pc(14), A.subtract)
    ts(pc(19), pc(15), 1.0e9, A.mult)
    tt(pc(20), pc(18), pc(19), A.add)
    ts(pc(21), pc(1), -2.0, A.mult, 1.0, A.add)
    tt(pc(22), pc(21), pc(13), A.mult)
    ts(pc(23), pc(15), -1.0, A.mult, 1.0, A.add)
    ts(pc(28), pc(0), -LN2, A.mult)
    ts(pc(29), pc(0), -LN2, A.mult, -16.0 * LN2, A.add)
    ts(pc(24), pc(1), -1.0, A.mult, 1.0, A.add)
    ts(pc(25), pc(0), 0.0, A.is_equal)
    ts(pc(26), pc(25), 4096.0, A.mult)
    sel(X("ta", 0, 128), X("ones", 0, 128), [[-16, 8], [0, 16]], A.is_ge, 0, 1)
    sel(X("BLKb"), X("ta", 0, 128), [[16, 8], [0, 16]], A.is_ge, 15, -1)
    for n, j in (("VW", 17), ("ALT", 22)):
        ts(X(n), X("BLKb"), pc(j), A.mult)
    for n, b in (("D0", 0), ("D2", 2), ("CA", -15), ("CB", -14), ("D1", 1)):
        sel(X(n), X("BLKb"), [[-1, 128]], A.is_equal, b, 1)
    ts(X("In"), X("D0"), -1.0, A.mult)
    ts(X("D0n"), X("D0"), pc(23), A.mult)
    tt(X("KE"), X("D0n"), X("ALT"), A.add)
    tt(X("KO"), X("D0n"), X("ALT"), A.subtract)
    tt(X("mt"), X("CA"), X("D0n"), A.subtract)
    tt(X("M2a"), X("D2"), X("CB"), A.add)
    tt(X("M2"), X("M2a"), X("mt"), A.add)
    tt(X("M1"), X("D1"), X("mt"), A.add)
    sel(X("ta"), X("ones"), [[-16, 9], [0, 16]], A.is_ge, 0, 1)
    sel(X("tb"), X("ta"), [[16, 9], [0, 16]], A.is_ge, 15, -1)
    sel(X("ZZ"), X("tb"), [[0, 9], [1, 16]], A.is_equal, -15, 0)
    iota(X("rr"), [[0, 16], [1, 16]], 0, 0)
    iota(X("tr"), [[16, 16]], W - 1536, 0)
    iota(X("idW"), [[1, W]], -1536, 0)
    cp(X("VL0"), X("pvI"))

    def more_consts():
        ts(X("ZFe"), X("ZZ"), pc(24), A.mult)
        ts(X("ZFo"), X("ZZ"), pc(1), A.mult)
        cp(X("ZFa"), X("ZZ"))
        ts((T.TRI[:, :, :], "TRI", 0, 256), X("rr"), pc(0), A.is_gt)
        ts(X("ZF0"), X("ZZ"), pc(25), A.mult)
        ts(X("ZB0"), X("ZZ"), pc(26), A.mult)
        ts(X("Ih"), X("D0"), 0.5, A.mult)
        ts(X("B7"), X("BLKb"), 0.4375, A.mult)
        cp(X("BF1"), X("BLKb"))
        ts(X("BFh"), X("BLKb"), 0.5, A.mult)
        ts(X("BF15"), X("BLKb"), pc(15), A.mult)
        ts(X("trS"), X("tr"), pc(0), A.add)
        cp(X("thF"), X("thI"))
        cp(X("Hc", 0, 1), X("thF", 0, 1))
        ts(X("bB"), X("thF", 1, 2), 2.0, A.mult, -1.0, A.add)

    nxt = T.cores[(rank + 1) % len(T.cores)]
    prv = T.cores[(rank - 1) % len(T.cores)]
    adr = topo.addr(nxt)
    eng = topo.engines(core, nxt)
    half = len(eng) // 2
    msk = sum(1 << e for e in eng[:half])
    n_in = len(topo.engines(prv, core)) // 2
    loc = [0]

    def send(dst, src, sem):
        deps = {}
        need("G", src[1], src[2], src[3], False, deps)
        waits("G", deps)
        g.remote_dma(dst, src[0], T.sem[sem], T.sem.loc, adr[1], adr[0], msk)
        loc[0] += half

    def arrive(t):
        rec["VL%d" % t] = [(0, 16, "R", "al%d" % t, n_in, True)]
        rec["VB%d" % t] = [(0, 256, "R", "av%d" % t, n_in, True)]
        rec["z%d" % t] = [(0, 128, "R", "ay%d" % t, n_in, True), (128, 256, "R", "az%d" % t, n_in, True)]

    def expand(copy, dst, src, i0, i1):
        a, b = 16 * i0, 16 * i1
        copy(X(dst, a, b, 16), X(src, i0, i1))
        for k in (8, 4, 2, 1):
            copy(X(dst, a + k, b, 2 * k), X(dst, a, b, 2 * k))

    def targets(t, c):
        expand(scp, "zE", "z%d" % t, 64 * c, 64 * c + 64)

    def ind_x(off):
        return IND(X("xdS", 0, W), off)

    def ind_n(off):
        return IND(X("nbS", 0, W), off)

    def erow(E, q):
        return (T[E][:, q, 0:256 - 16 * q], E, 256 * q, 240 * q + 256)

    def count(ps, lhs, E):
        mms([(X(ps, 16 * q, 256), lhs(q), erow(E, q)) for q in range(16)])

    def to_list(ps, src):
        mms([(X(ps, 480, 496), X("ZB0", 15 - r, 143 - r), X(src, r, 256, 16)) for r in range(16)])

    def place(ps, src, out):
        tt(X("o1"), X(ps, 480, 496), X(src), A.add)
        tt(X("o2"), X("o1"), X("trS"), A.min)
        ts(X(out), X("o2"), 1536.0, A.add)

    def new_contacts():
        nw = X("ps0", 0, 256)
        tt(nw, nw, X("conF"), A.subtract)
        tt(nw, nw, X("ohb"), A.mult)
        tt(X("wv"), nw, X("conF"), A.add)

    for t in range(4):
        VL, VB, z, E, pk = "VL%d" % t, "VB%d" % t, "z%d" % t, "E3%d" % (t % 2), "pk%d" % t
        last = t == 3

        if t == 0:
            targets(0, 0)
        tt(X("dz"), ind_x(X(VL)), X(z), A.subtract)
        ts(X("nn"), X("dz"), 1.0, A.is_gt)
        ts(X("nm"), X("dz"), -1.0, A.is_lt)
        mms([(X("ps6", 0, 256), X("VW"), X("nn")), (X("ps6", 0, 256), X("VW"), X("nm"))])
        act(X("adz"), X("dz"), F.Abs)
        mms([(X("ps5", 0, 256), X("D0"), X("adz")), (X("ps5", 0, 256), X("In"), X(z))])
        if not last:
            ts(X("xi"), X("dz"), 0.5, A.mult, 191.75, A.add)
            mms([(X("ps5", 256, 512), X("D0"), X("xi")), (X("ps5", 256, 512), X("D0"), X(z))])
        if t > 0:
            new_contacts()
            place("ps2", "o3", "offR")
        else:
            targets(0, 1)
        targets(t, 2)
        scp(X("dlt"), X("ps5", 0, 256))
        if not last:
            act(X("xn"), X("ps5", 256, 512), F.Copy, bias=-192.0)
        ts(X("Pb"), X("ps6", 0, 256), pc(20), A.is_lt)
        mms([(X("ps1", 0, 256), X("M2"), X("Pb"))])
        mms([(X("ps1", 256, 512), X("M1"), X("Pb"))])
        mms([(X("ps6", 0, 256), X("KE"), X("Pb"))])
        mms([(X("ps6", 256, 512), X("KO"), X("Pb"))])
        scp(X("m2"), X("ps1", 0, 256))
        ts(X("vS"), X(VL), -1536.0, A.add)
        if t == 0:
            more_consts()
            for j in range(4):
                a, b = j * C4, (j + 1) * C4
                ts(X("nbS", a, b), X("nbI", a, b), -1536.0, A.add)
        else:
            cp(IND(X("nbS", 0, WT), X("offR")), X("wv"))
        ts(X("conU"), ind_n(X(VL)), 1536.0, A.add)
        expand(cp, "maskE", "m2", 0, 64)
        for c in range(1, 4):
            expand(scp, "maskE", "m2", 64 * c, 64 * c + 64)
            if c == 1:
                act(X("conF"), ind_n(X(VL)), F.Copy)

        def gather_nb(c):
            s = 1024 * c
            tt(X("mk", s, s + 1024), ind_n(X("conU", 64 * c, 64 * c + 64)), X("maskE", s, s + 1024), A.mult)
            for par, zz in ((0, "ZFe"), (1, "ZFo")):
                col = par * 128 + (c % 2) * 64
                mms([(X("ps%d" % (3 + c // 2), col, col + 64), X(zz, 15 - k, 143 - k), X("mk", s + k, s + 1024, 16))
                     for k in range(16)])

        def lists(h):
            ts(X("cU", 256 * h, 256 * h + 256), X("ps%d" % (3 + h), 0, 256), 1536.0, A.add)

        gather_nb(0)
        gather_nb(1)
        tt(X("co"), X("ps1", 256, 512), X("conF"), A.mult)
        cp(X("ohb"), X("ps1", 256, 512))
        mms([(X("ps2", 0, 16), X("ZFa", 15 - r, 143 - r), X("co", r, 256, 16)) for r in range(16)])
        for par in range(2):
            act((T.Wt[:, :, 128 * par:128 * par + 128], "Wt", 0, 512), X("ps6", 256 * par, 256 * par + 256), F.Exp,
                bias=pc(28 + par), scale=-16.0 * LN2)
        gather_nb(2)
        lists(0)
        ts(X("TLu"), X("ps2", 0, 16), 1536.0, A.add)
        gather_nb(3)
        targets(t, 3)

        def dsum(c, par):
            s = 1024 * (2 * c + par)
            col = par * 128 + (c % 2) * 64
            mms([(X("ps%d" % (5 + c // 2), col, col + 64), X("ZZ", 15 - k, 143 - k), X("dd", s + k, s + 1024, 16)) for k in range(16)])

        def ccols(c, par):
            col = 256 * (c // 2) + par * 128 + (c % 2) * 64
            return X("cU", col, col + 64)

        def raw(c):
            act(X("xg", 1024 * c, 1024 * c + 1024), ind_x(ccols(c, 1)), F.Copy)

        def raw_sub(c):
            for b in range(2):
                a0 = 1024 * c + 512 * b
                mms([(X("ps%d" % b), X("D0"), X("xg", a0, a0 + 512)), (X("ps%d" % b), X("In"), X("zE", a0, a0 + 512))])

        def raw_abs(c):
            s = 1024 * (2 * c + 1)
            for b in range(2):
                act(X("dd", s + 512 * b, s + 512 * b + 512), X("ps%d" % b), F.Abs)
            dsum(c, 1)

        def cand(c, par):
            s = 1024 * (2 * c + par)
            tt(X("dd", s, s + 1024), ind_x(ccols(c, par)), X("zE", 1024 * c, 1024 * c + 1024), A.subtract)
            act(X("dd", s, s + 1024), X("dd", s, s + 1024), F.Abs)
            dsum(c, par)

        def pairs():
            if t == 0:
                cp(X(VB), IND(X("idW"), X(VL)))
            for q in range(16):
                ts(erow(E, q), X(VB, 16 * q, 256), X("vS", q, q + 1), A.is_equal)
            diag = (T[E][:, :, 0:16], E, 0, 4096)
            tt(diag, diag, (T.TRI[:, :, :], "TRI", 0, 256), A.mult)

        def relu(h):
            act(X("ps%d" % (5 + h), 0, 256), X("ps%d" % (5 + h), 0, 256), F.Relu, bias=X("bB"), scale=-2.0)

        raw(0)
        raw_sub(0)
        raw(1)
        cand(0, 0)
        raw_abs(0)
        raw_sub(1)
        lists(1)
        pairs()
        if not last:
            count("ps2", lambda q: X("BLKb"), E)
        raw(2)
        tt(X("d0"), ind_x(X("TLu")), X(z), A.subtract)
        act(X("d0"), X("d0"), F.Abs)
        mms([(X("ps7", 256, 512), X("BLKb"), X("d0"))])
        raw_abs(1)
        raw_sub(2)
        cand(1, 0)
        if not last:
            scp(X("cb"), X("ps2", 0, 256))
            to_list("ps2", "cb")
        cand(2, 0)
        raw_abs(2)
        hb = X("ps7", 256, 512)
        ts(hb, hb, X("Hc", t, t + 1), A.is_lt, 2.0, A.mult)
        tt(X("hc"), hb, X("co"), A.mult)
        relu(0)
        act(X("hb2"), hb, F.Copy, acc=X("hs", t, t + 1))
        cand(3, 0)

        def tail_a(h):
            tt(X("hw", 256 * h, 256 * h + 256), X("ps%d" % (5 + h), 0, 256), (T.Wt[:, h, :], "Wt", 256 * h, 256 * h + 256), A.min)
            s = X("ps7", 128 * h, 128 * h + 128)
            mms([(s, X("B7"), X("hw", 256 * h, 256 * h + 128)), (s, X("B7"), X("hw", 256 * h + 128, 256 * h + 256)),
                 (s, X("Ih"), X("hb2", 128 * h, 128 * h + 128))])

        def tail_b(h):
            a, b = 128 * h, 128 * h + 128
            s = X("ps7", a, b)
            for par in range(2):
                u = 256 * h + 128 * par
                tt(X("fi", u, u + 128), X("hw", u, u + 128), s, A.is_gt)
            tt(X("fc", 256 * h, 256 * h + 256), X("ps%d" % (3 + h), 0, 256), X("fi", 256 * h, 256 * h + 256), A.mult)
            lo = X("ps1", 256 + a, 256 + b)
            ts(lo, s, 0.0, A.is_equal)
            tt(X("lc", a, b), lo, X("conF", a, b), A.mult)
            o = X("ps0", a, b)
            mms([(o, X("BFh"), X("hc", a, b)), (o, X("BF1"), X("fc", 256 * h, 256 * h + 128)),
                 (o, X("BF1"), X("fc", 256 * h + 128, 256 * h + 256)), (o, X("BF15"), X("lc", a, b))])
            tt(lo, lo, X("dlt", a, b), A.mult)
            zn = X("zn%d" % t, a, b)
            tt(zn, lo, X(z, a, b), A.add)
            if not last:
                send(T["z%d" % (t + 1)][:, a:b], zn, ("ay%d" if h == 0 else "az%d") % (t + 1))
            else:
                dma("Y", T.yz[:, a:b], [], zn[0], [zn], "yz%d" % h)
            tt(X(pk, 256 + a, 256 + b), s, X("hb2", a, b), A.is_gt)

        def weigh(qs, on_scalar):
            for q in qs:
                if on_scalar:
                    act(X("LQ", 128 * q, 128 * q + 128), X("BLKb"), F.Copy, scale=X("rp", q, q + 1))
                else:
                    ts(X("LQ", 128 * q, 128 * q + 128), X("BLKb"), X("rp", q, q + 1), A.mult)

        tail_a(0)
        cand(3, 1)
        relu(1)
        if last:
            act(X("yn", 0, W), X("nbS", 0, W), F.Copy, bias=1536.0)
        tail_b(0)
        if not last:
            place("ps2", "vS", "offA")
            scp(X("hsb", t, t + 1), X("hs", t, t + 1))
            mms([(X("ps4", 256, 257), X("AW"), X("hsb", t, t + 1))])
        tail_a(1)
        cp(X(pk, 0, 128), X("ps0", 0, 128))
        tail_b(1)
        cp(X(pk, 128, 256), X("ps0", 128, 256))
        mms([(X("ps5", 256, 288), X("ZF0", 15 - r, 143 - r), X(pk, r, 512, 16)) for r in range(16)])
        if not last:
            ts(X("hi0", t, t + 1), X("ps4", 256, 257), -1.0, A.mult, 2048.0, A.add)
            ts(X("hi1", t, t + 1), X("hi0", t, t + 1), 15, A.bitwise_and)
            tt(X("Hc", t + 1, t + 2), X("hi1", t, t + 1), X("thF", 0, 1), A.add)
        ts(X("VN%d" % t if not last else "yvS"), X("ps5", 256, 272), 1536.0, A.add)
        if not last:
            send(T["VL%d" % (t + 1)][:, :], X("VN%d" % t), "al%d" % (t + 1))
            send(T["VB%d" % (t + 1)][:, :], X(pk, 0, 256), "av%d" % (t + 1))
            arrive(t + 1)
            targets(t + 1, 0)
        else:
            dma("Y", T.yv[:, :], [], T.yvS[:, :], [X("yvS")], "yv")
        scp(X("rp"), X("ps5", 272, 288))
        weigh(range(0, 10), False)
        weigh(range(10, 16), True)
        count("ps2", lambda q: X("LQ", 128 * q, 128 * q + 128), E)
        if not last:
            cp(IND(X("xdS", 0, WT), X("offA")), X("xn"))
            targets(t + 1, 1)
        ts(X("q1"), X("rp"), -4096.0, A.mult, 4096.0, A.add)
        tt(X("o3"), X("q1"), X("vS"), A.add)
        scp(X("crb"), X("ps2", 0, 256))
        to_list("ps2", "crb")
    new_contacts()
    place("ps2", "o3", "offR")
    ot = IND(X("yn", 0, WT), X("offR"))
    op("V", lambda e: e.tensor_scalar(ot[0], T.wv[:, :], 1.0, 1536.0, A.mult, A.add), [X("wv"), ot[2]], [ot[1]])

    for j in range(4):
        a, b = j * C4, (j + 1) * C4
        dma("Y" if j % 2 == 0 else "S", T.ynb[:, a:b], [], T.yn[:, a:b], [X("yn", a, b)], "y%d" % j)
    fin = {s: cnt[s] for s in cnt}
    for d in DMAS:
        fin["d_" + d] = 16
    fin["loc"] = loc[0]
    for s in fin:
        if known["G"].get(s, 0) < fin[s]:
            g.wait_ge(T.sem[s], fin[s])
